import numpy as np, ml_dtypes
CORES = [13,21,141,149]
N = 4
BF = ml_dtypes.bfloat16
def gentries(a):
    return np.ascontiguousarray(a.reshape(8, 16, -1).transpose(0, 2, 1)).reshape(8, -1)
def gtable(e):
    e = np.asarray(e); return np.ascontiguousarray(e.reshape(8, -1, 16).transpose(0, 2, 1)).reshape(128, -1).astype(np.int32)
W, NW, P, RO, F = 4096, 128, 32, 3, 2
S = W // NW
def parts(rng):
    x = rng.integers(0, 16, (N, 8, 16, W)); l = rng.integers(0, W, (N, 8, NW, P))
    n = np.where(rng.random((N, 8, NW)) < 0.12, rng.integers(0, P + 1, (N, 8, NW)), rng.integers(P // 2, P + 1, (N, 8, NW)))
    return x, l, n, rng.integers(0, 256, (N, 8, 16)), rng.integers(68, 100, (N, 8))
def pack(x, l, n, w, t):
    return {"xv": np.ascontiguousarray(x.reshape(N, 128, W)).astype(np.float32).astype(BF), "wl": np.stack([gtable(a.reshape(8, NW * P)) for a in l]),
            "wn": np.ascontiguousarray(n).astype(np.int32), "wt": np.ascontiguousarray(w.reshape(N, 128, 1)).astype(np.int32), "th": np.ascontiguousarray(t.reshape(N, 8, 1)).astype(np.int32)}
def setup_inputs(rng):
    return pack(*parts(rng))
def setup_inputs_alike(rng):
    x, l, n, w, t = parts(rng)
    l[:, ::2] = rng.choice(np.array([0, W - 1, W // 2, 3]), (N, 4, NW, P))
    l[:, 1] = l[:, 1, :, :1]; x[:, 3] = x[:, 3, :, :1]; w[:, 5] = 0; n[:, 6] = P; t[:, 7] = 0
    return pack(x, l, n, w, t)
def setup_inputs_corners(rng):
    x, l, n, w, t = parts(rng); k = np.arange(P)
    x = rng.integers(0, 4, (N, 8, 16, W)) + 12 * (np.arange(W) & 1); t = rng.integers(48, 144, (N, 8)); t[:, 0] = 48; t[:, 7] = 143
    w = np.where(rng.random((N, 8, 1)) < 0.3, 255 * rng.integers(0, 2, (N, 8, 1)), w)
    n = rng.choice(np.array([0, 1, 2, P - 1, P, P, P, P]), (N, 8, NW)); m = np.minimum(n, rng.choice(np.array([1, 2, P // 2, P // 2 + 1, P - 1, P]), (N, 8, NW)))
    pick = rng.random((8, NW)) < 0.4; a = rng.integers(P // 2, P + 1, (8, NW)); a[:, 0] = P // 2 + 1; a[:, NW - 1] = P; pick[:, 0] = True; pick[:, NW - 1] = True
    for q in range(0, N - 1, 2):
        m[q] = np.where(pick, a, m[q]); n[q] = np.where(pick, np.maximum(a, rng.integers(0, P + 1, (8, NW))), n[q])
        m[q + 1] = np.where(pick, P - a, m[q + 1]); n[q + 1] = np.where(pick, np.where(a == P, 0, np.maximum(P - a, rng.integers(1, P + 1, (8, NW)))), n[q + 1])
    m[0, 5] = P; n[0, 5] = P; m[1, 4] = 0; n[1, 4] = 0
    m[N - 2] = P; n[N - 2] = P; m[N - 1] = 0; n[N - 1] = 0
    for q in (0, 1):
        fr = np.where(pick, 0, m[q]); fr[5] = 0; fr = fr.reshape(-1); o = rng.permutation(8 * NW); b = fr[o]; cut = np.zeros_like(b)
        cut[o] = np.clip((int(np.sum(m[q])) - 256) % 512 - (np.add.accumulate(b) - b), 0, b)
        m[q] = m[q] - cut.reshape(8, NW); n[q] = np.where(m[q] == 0, 0, n[q])
    sc = np.where((k == 0) | (k >= n[..., None]), 2.0, rng.random((N, 8, NW, P)))
    brk = np.argsort(np.argsort(sc, axis=-1), axis=-1) < (m - 1)[..., None]
    cl = (rng.integers(0, 2, (N, 8, NW, 1)) + np.add.accumulate(brk.astype(np.int64), axis=-1)) & 1
    l = np.where(rng.random((N, 8, NW, P)) < 0.1, cl * (W - 1), 2 * rng.integers(0, W // 2, (N, 8, NW, P)) + cl)
    return pack(x, l, n, w, t)
def setup_inputs_ends(rng):
    kind = rng.integers(0, 3, (N, 8, 1, W)); k = np.arange(P); c = np.arange(1, P + 1)
    x = np.where(kind == 0, 0, np.where(kind == 1, 15, 15 * rng.integers(0, 2, (N, 8, 16, W))))
    for u, v in ((0, 15), ((240 * 255) & (W - 1), 0)):
        hh = ((u * u >> 5) + 37 * u + 611 * c) & (W - 1)
        for g in (0, 7): x[:, g][..., hh] = v
    x[..., 0] = 0; x[..., W - 1] = 15
    w = 255 * rng.integers(0, 2, (N, 8, 16)); w[:, 0] = 255; w[:, 7] = 255; w[:, 3, 0] = 0; w[:, 4] = 0
    t = 239 * rng.integers(0, 2, (N, 8)); t[:, 0] = 0; t[:, 1] = 239; t[:, 7] = 239
    kd = rng.integers(0, 4, (N, 8, NW, 1)); s = rng.integers(0, 2, (N, 8, NW, 1)); em = np.where(np.arange(N) == N - 1, 0.05, 0.25).reshape(N, 1, 1)
    kd[N - 1] = np.where(rng.random((8, NW, 1)) < 0.9, 1, kd[N - 1]); kd[:, :, 0] = 1; kd[:, 7, NW - 1] = 1; kd[:, 7, NW - 2] = 0; s[:, 7, NW - 2] = 1
    b = np.where(kd == 0, s, np.where(kd == 1, (k + s) & 1, rng.integers(0, 2, (N, 8, NW, P))))
    n = P * (rng.random((N, 8, NW)) > em).astype(np.int64); n[:, :, 0] = P; n[:, :, 1] = 0; n[:, :, NW - 2] = P; n[:, :, NW - 1] = P
    return pack(x, (W - 1) * b, n, w, t)
def setup_inputs_spread(rng):
    x, l, n, w, t = parts(rng)
    x = (rng.random((N, 8, 16, W)) * np.exp2(rng.integers(0, 5, (N, 8, 1, W)))).astype(np.int64)
    l = np.minimum((W * rng.random((N, 8, NW, P)) ** rng.choice(np.array([0.3, 1.0, 3.0]), (N, 8, 1, 1))).astype(np.int64), W - 1)
    n = rng.integers(0, P + 1, (N, 8, NW)); w = (256 * rng.random((N, 8, 16)) ** 2).astype(np.int64)
    t = np.exp2(7.9 * rng.random((N, 8))).astype(np.int64) - 1
    return pack(x, l, n, w, t)
def setup_inputs_ties(rng):
    x, l, n, w, t = parts(rng)
    lane = np.argsort(rng.random((N, 8, 16)), axis=-1); pm = np.argsort(rng.random((N, 8, W)), axis=-1)
    lev = np.zeros((N, 8, W), np.int64); np.put_along_axis(lev, pm, np.broadcast_to(np.arange(W) % 241, (N, 8, W)), 2)
    x = np.clip(lev[:, :, None, :] - 15 * lane[..., None], 0, 15)
    t = rng.choice(np.array([0, 1, 15, 16, 47, 80, 100]), (N, 8)); s = rng.integers(0, 241, (N, 8, NW))
    for k in range(P):
        l[..., k] = np.take_along_axis(pm, s + 241 * rng.integers(0, W // 241, (N, 8, NW)), 2)
        st = np.abs(t[:, :, None] + rng.integers(-1, 2, (N, 8, NW))); up = ((rng.random((N, 8, NW)) < 0.5) & (s + st <= 240)) | (s - st < 0)
        s = np.where(up, s + st, s - st)
    t[:, 7] = 239
    hl = 239 * ((np.arange(P) + rng.integers(0, 2, (N, NW, 1))) & 1) + rng.integers(0, 2, (N, NW, P)) + 241 * rng.integers(0, W // 241, (N, NW, P))
    l[:, 7] = np.take_along_axis(pm[:, 7], hl.reshape(N, NW * P), 1).reshape(N, NW, P)
    return pack(x, l, n, w, t)
def check_inputs(d):
    bad = []
    for k, lo, hi in (("xv", 0, 15), ("wl", 0, W - 1), ("wn", 0, P), ("wt", 0, 255), ("th", 0, 239)):
        v = np.asarray(d[k]).astype(np.float64)
        if not (np.min(v) >= lo and np.max(v) <= hi): bad.append("range of " + k)
        elif np.any(v != np.floor(v)): bad.append("whole numbers of " + k)
    return bad
def reference(xv, wl, wn, wt, th):
    x = xv.astype(np.int32).reshape(N, 8, 16, W); w = wt.astype(np.int32).reshape(N, 8, 16, 1, 1); lim = th.astype(np.int64).reshape(N, 8, 1, 1)
    l = np.stack([gentries(a) for a in wl]).astype(np.int64).reshape(N, 8, NW, P); n = wn.astype(np.int64)
    last = np.zeros((N, 1, 1, 1), np.int64); k = np.arange(P); M = W - 1
    for t in range(RO):
        if t > 0:
            l = np.roll(l, (1, 1), axis=(0, 1)); n = np.roll(n, (1, 1), axis=(0, 1))
        live = k < n[..., None]
        v = np.take_along_axis(x, l.reshape(N, 8, 1, NW * P), 3).reshape(N, 8, 16, NW, P)
        dist = np.add.reduce(np.abs(v[..., 1:] - v[..., :-1]), axis=2)
        start = live.copy(); start[..., 1:] &= dist > lim
        end = live.copy(); end[..., :-1] &= start[..., 1:] | ~live[..., 1:]
        num = np.add.accumulate(start.astype(np.int64), axis=-1) - 1; m = np.add.reduce(start.astype(np.int64), axis=-1)
        z = v.copy(); c = np.ones((N, 8, NW, P), np.int64); f = l.copy()
        for j in range(1, P):
            s = start[..., j]
            z[..., j] = np.where(s[:, :, None], v[..., j], np.maximum(z[..., j - 1], v[..., j]))
            c[..., j] = np.where(s, 1, c[..., j - 1] + 1); f[..., j] = np.where(s, l[..., j], f[..., j - 1])
        u = np.add.reduce(w * z, axis=2).astype(np.int64) & M
        h = ((u * u >> 5) + 37 * u + 611 * c) & M
        xh = np.take_along_axis(x, h.reshape(N, 8, 1, NW * P), 3).reshape(N, 8, 16, NW, P)
        dd = np.add.reduce(np.abs(xh - z), axis=2).astype(np.int64)
        y = np.zeros((N, 8, NW, 2 * P + 2), np.int64)
        np.put_along_axis(y, np.where(end, 2 * num, 2 * P), ((f * (2 * c + 1) >> 2) + last) & M, 3)
        np.put_along_axis(y, np.where(end, 2 * num + 1, 2 * P + 1), (h + dd * (2 * c + 1)) & M, 3)
        own = np.minimum(2 * m, P); over = np.roll(2 * m - own, 1, axis=0); oy = np.roll(y[..., P:2 * P], 1, axis=0)
        n = np.minimum(own + over, P); o = own[..., None]
        l = np.where(k < o, y[..., :P], np.where(k < n[..., None], np.take_along_axis(oy, np.clip(k - o, 0, P - 1), 3), 0))
        e = np.argmax(end, axis=-1)[..., None]; e5 = e[:, :, None]
        val = ((np.take_along_axis(z, e5, 4) + np.take_along_axis(xh, e5, 4)) >> 1)[..., 0]
        at = (S * np.arange(NW) + (np.take_along_axis(u, e, 3)[..., 0] & (S - 1)))[:, :, None]
        np.put_along_axis(x, at, np.where((m > 0)[:, :, None], val, np.take_along_axis(x, at, 3)), 3)
        last = np.add.reduce(m.reshape(N, 8 * NW), axis=1).reshape(N, 1, 1, 1) & 255
    return {"yx": np.add.reduce(x.reshape(N, 128, W // F, F), axis=3).astype(np.float32).astype(BF), "yl": np.stack([gtable(a.reshape(8, NW * P)) for a in l]).astype(np.float32), "yn": n.astype(np.float32)}

@@ -1,0 +1,666 @@
+import numpy as np
+from concourse.bass import DstId, RemoteDMATransfer
+from concourse.mybir import dt, AluOpType, AxisListType, ActivationFunctionType
+
+NW, P, RO = 128, 32, 3
+NB = 64
+NBK = NW // NB
+W = 4096
+DEAD = 4096
+ROWS = P * NB
+CH = 512
+AF = ActivationFunctionType
+OP = AluOpType
+
+SCRATCH = {}
+for _i in range(8):
+    SCRATCH["ps%d" % _i] = ("psum", [128, 512], "float32")
+
+
+SIZE, PLACE, FILL = {}, {}, {"float32": 0, "int32": 0, "uint16": 0, "bfloat16": 0}
+OWN = ("XT", "wli", "wni", "thi", "wti", "YX", "snd", "rcv", "mos", "mor", "yl3", "yno")
+
+
+def _sb(name, n, dtype):
+    SIZE[name] = (n, dtype)
+    if name[:3] in OWN or name in OWN:
+        SCRATCH[name] = ("sbuf", [128, n], dtype)
+        PLACE[name] = (name, 0)
+    else:
+        PLACE[name] = ("all_" + dtype, FILL[dtype])
+        FILL[dtype] += -(-n // 16) * 16
+
+
+_sb("XT", W + 16 + 128, "bfloat16"); _sb("DG", W + 16, "bfloat16"); _sb("LUT", 768, "bfloat16"); _sb("QW", 4096, "bfloat16")
+_sb("wli", 2 * NW, "int32"); _sb("wni", NW, "int32"); _sb("thi", 1, "int32"); _sb("wti", 1, "int32")
+_sb("wnf", NW + 1, "float32"); _sb("E8", 128, "float32"); _sb("nr0", NW + 1, "float32")
+_sb("pint", 1, "int32"); _sb("lani", 1, "int32"); _sb("grpi", 1, "int32"); _sb("roti", 1, "int32"); _sb("rotj", 1, "int32")
+_sb("cols", 40, "float32")
+_sb("XR", 144, "float32"); _sb("GR", 128, "float32"); _sb("YI", 52, "float32"); _sb("IO", NB, "float32")
+_sb("WI", 8, "float32"); _sb("WI1", 8, "float32"); _sb("WI2", 8, "float32")
+_sb("DD", 256, "bfloat16"); _sb("DB", 256, "bfloat16"); _sb("DD2", 256, "bfloat16"); _sb("DB2", 256, "bfloat16"); _sb("DP", 256, "bfloat16")
+_sb("A16", 16, "float32"); _sb("A16b", 16, "float32")
+_sb("VY", 52, "bfloat16"); _sb("VY1", 52, "bfloat16"); _sb("VY2", 52, "bfloat16")
+_sb("ID", 128, "bfloat16"); _sb("NEG", 128, "bfloat16"); _sb("BLK", 128, "bfloat16"); _sb("BLK2", 128, "bfloat16"); _sb("BL16", 128, "bfloat16")
+_sb("EW", 144, "bfloat16"); _sb("WW", 144, "bfloat16"); _sb("DW", 144, "bfloat16"); _sb("L0W", 144, "bfloat16")
+for _i in range(4):
+    _sb("SE%d" % _i, 144, "bfloat16"); _sb("PM%d" % _i, 128, "float32")
+_sb("GT", 1024, "bfloat16"); _sb("TBf", 128, "float32"); _sb("AS", 128, "float32"); _sb("ROT", 128, "float32"); _sb("ROT4", 128, "float32")
+_sb("IDF", 128, "float32"); _sb("IDF4", 128, "float32"); _sb("BIG", 128, "bfloat16"); _sb("ONE", CH // P, "bfloat16"); _sb("P8", 8, "float32")
+_sb("NLi", 2 * NW, "float32"); _sb("NLf", 2 * NW, "float32"); _sb("NL", 2 * NW, "uint16")
+_sb("MS", NBK, "float32"); _sb("AT", 1, "float32"); _sb("ATi", 1, "int32"); _sb("ATj", 1, "int32"); _sb("AC", 4, "float32")
+_sb("ZF", NW, "bfloat16"); _sb("VAL", NW, "bfloat16")
+for _n, _d in (("wa", "int32"), ("wb", "int32"), ("wc", "float32"), ("wd", "float32"), ("we", "float32"), ("wf", "float32")):
+    _sb(_n, 8, _d)
+_sb("WL", 8, "uint16"); _sb("YX", 2048, "bfloat16")
+for _b in range(NBK):
+    _s = str(_b)
+    _sb("V" + _s, ROWS + 16, "bfloat16"); _sb("B" + _s, ROWS + 16, "bfloat16"); _sb("D" + _s, ROWS, "bfloat16")
+    _sb("C" + _s, ROWS, "bfloat16"); _sb("Z" + _s, ROWS, "bfloat16")
+    _sb("n" + _s, NB, "float32"); _sb("is" + _s, NB, "float32"); _sb("m" + _s, NB, "float32"); _sb("IB" + _s, NB, "float32")
+    _sb("mg" + _s, 2 * NB, "float32"); _sb("nm" + _s, 2 * NB, "uint16"); _sb("pv" + _s, NB, "bfloat16")
+    _sb("e2" + _s, NB, "int32"); _sb("io" + _s, NB, "float32")
+    _sb("yl1" + _s, 2 * NB, "float32"); _sb("yl2" + _s, 2 * NB, "float32"); _sb("yl3" + _s, 2 * NB, "float32"); _sb("yno" + _s, NB, "float32")
+    for _t in range(RO):
+        _sb("mos%d%d" % (_t, _b), NB, "bfloat16"); _sb("mor%d%d" % (_t, _b), NB, "bfloat16")
+        for _h in (0, 1):
+            _sb("snd%d%d%d" % (_t, _b, _h), 2 * NB, "float32"); _sb("rcv%d%d%d" % (_t, _b, _h), 2 * NB, "float32")
+    for _h in (0, 1):
+        _s = "%d%d" % (_b, _h)
+        for _n, _k, _d in (("ix", NB, "uint16"), ("G", 16 * NB, "bfloat16"), ("Pi", NB, "int32"), ("ci", NB, "int32"), ("si", NB, "int32"),
+                           ("af", NB, "float32"), ("ao", NB, "uint16"), ("zf", NB, "float32"), ("zo", NB, "uint16"), ("iv", NB, "float32"),
+                           ("iw", NB, "float32"), ("iy", NB, "float32"), ("c2", NB, "float32"), ("c6", NB, "float32"), ("Zc", 16 * NB, "bfloat16"),
+                           ("Ac", 16 * NB, "bfloat16"), ("t1", NB, "float32"), ("t2", NB, "float32"), ("ui", NB, "int32"), ("um", NB, "int32"),
+                           ("sq", NB, "int32"), ("qq", NB, "int32"), ("hh", NB, "int32"), ("hm", NB, "int32"), ("hu", NB, "uint16"),
+                           ("D2", 16 * NB, "bfloat16"), ("AD", 16 * NB, "bfloat16"), ("na", NB, "float32"), ("nc", NB, "float32"),
+                           ("NN", 2 * NB, "int32"), ("NM", 2 * NB, "int32"), ("NF", 2 * NB, "float32")):
+            _sb(_n + _s, _k, _d)
+for _i in range(8):
+    SIZE["ps%d" % _i] = (512, "float32"); PLACE["ps%d" % _i] = ("ps%d" % _i, 0)
+for _d in FILL:
+    SCRATCH["all_" + _d] = ("sbuf", [128, FILL[_d]], _d)
+
+SEMAPHORES = ["sv", "sa", "st", "sg", "loc"]
+SEMAPHORES += ["d%d" % i for i in range(6 + 2 * NBK)]
+for _t in range(RO):
+    for _b in range(NBK):
+        SEMAPHORES += ["mo%d%d" % (_t, _b), "nm%d%d0" % (_t, _b), "nm%d%d1" % (_t, _b)]
+
+CY = 0.00083
+HOP1, HOP2 = 3.5, 6.5
+LINK = 0.06
+VPEN = 0.0
+
+
+def messages(q, n):
+    out = []
+    for t in range(RO):
+        for b in range(NBK):
+            out.append(("mo", t, b, (q - 1) % n))
+            if t < RO - 1:
+                out.append(("own", t, b, (q + 1) % n))
+                out.append(("over", t, b, (q + 2) % n))
+            else:
+                out.append(("over", t, b, (q + 1) % n))
+    return out
+
+
+def names_of(kind, t, b):
+    if kind == "mo":
+        return "mos%d%d" % (t, b), "mor%d%d" % (t, b), "mo%d%d" % (t, b)
+    h = 1 if kind == "over" else 0
+    return "snd%d%d%d" % (t, b, h), "rcv%d%d%d" % (t, b, h), "nm%d%d%d" % (t, b, h)
+
+
+def relay_of(topo, src, dst, kind):
+    if topo.may_write(src, dst):
+        return None
+    c = [x for x in topo.cores_of(src) if x != src and topo.die(x) == topo.die(src) and topo.may_write(x, dst)]
+    return c[0] if kind != "mo" else c[-1]
+
+
+def emask(topo, src, dst, n=8):
+    m = 0
+    for e in topo.engines(src, dst)[:n]:
+        m |= 1 << e
+    return m, len(topo.engines(src, dst)[:n])
+
+
+def send(g, T, topo, core, dst, sbuf, dbuf, sem):
+    m, k = emask(topo, core, dst)
+    rid, pid = topo.addr(dst, core)
+    g.remote_dma(T[dbuf][:, :], T[sbuf][:, :], T.sem[sem], T.sem["loc"], pid, rid, m)
+    return k
+
+
+def relay_program(g, core, T, topo):
+    todo = []
+    n = len(T.cores)
+    for q in range(n):
+        for kind, t, b, d in messages(q, n):
+            dst = T.cores[d]
+            if relay_of(topo, T.cores[q], dst, kind) == core:
+                todo.append((t, kind == "over", b, kind, T.cores[q], dst))
+    tot = 0
+    for t, _, b, kind, src, dst in sorted(todo):
+        sb, lb, sem = names_of(kind, t, b)
+        g.wait_ge(T.sem[sem], emask(topo, src, core)[1])
+        tot += send(g, T, topo, core, dst, lb, lb, sem)
+    if tot:
+        g.wait_ge(T.sem["loc"], tot)
+
+
+def clash(a, b):
+    if a[0] != b[0]:
+        return False
+    if a[0][:2] == "ps":
+        return True
+    if a[2] <= b[1] or b[2] <= a[1]:
+        return False
+    if a[3] == b[3] and a[3] > 1 and (a[1] - b[1]) % a[3]:
+        return False
+    return True
+
+
+def rank_program(g, core, T, topo):
+    rank = T.rank_of(core)
+    if rank is None:
+        return relay_program(g, core, T, topo)
+    nr = len(T.cores)
+    nodes = []
+    hist = {}
+    eng = {"v": g.vector, "a": g.scalar, "p": g.tensor, "g": g, "s": g.sync}
+    esem = {"v": "sv", "a": "sa", "p": "st", "g": "sg"}
+
+    def add(e, dur, w, r, fn, sem=None, inc=1, after=(), lat=0.0):
+        i = len(nodes)
+        deps = {}
+        for x in r:
+            ps = x[0][:2] == "ps"
+            for (j, y, k) in hist.get(x[0], ()):
+                if (k or ps) and clash(x, y):
+                    deps[j] = 1
+        for x in w:
+            for (j, y, k) in hist.get(x[0], ()):
+                if clash(x, y):
+                    deps[j] = 1
+        for j in after:
+            deps[j] = 1
+        for x in w:
+            h = hist.setdefault(x[0], [])
+            h[:] = [z for z in h if not (x[3] == 1 and x[1] <= z[1][1] and z[1][2] <= x[2])] if x[0][:2] != "ps" else []
+            h.append((i, x, 1))
+        for x in r:
+            hist.setdefault(x[0], []).append((i, x, 1 if x[0][:2] == "ps" else 0))
+        banks = []
+        for x in list(w) + list(r):
+            if x[0][:2] == "ps" and x[0] not in banks:
+                banks.append(x[0])
+        if not isinstance(dur, dict):
+            dur, f1 = {e: dur}, fn
+            fn = lambda e: f1()
+        nodes.append({"e": e, "d": dur, "banks": banks, "w": w, "deps": sorted(deps), "fn": fn, "sem": sem, "inc": inc, "lat": lat})
+        return i
+
+    def A(r, rows=None):
+        n, o = ("ps%d" % phys[r[0]], 0) if r[0][:3] == "ps@" else PLACE[r[0]]
+        p = slice(None) if rows is None else slice(0, rows)
+        return T[n][p, o + r[1]:o + r[2]:r[3]] if r[3] > 1 else T[n][p, o + r[1]:o + r[2]]
+
+    def R(name, lo=0, hi=None, step=1):
+        return (name, lo, SIZE[name][0] if hi is None else hi, step)
+
+    def num(r):
+        return -(-(r[2] - r[1]) // r[3])
+
+    def two(r):
+        return r[0][:2] != "ps" and SIZE[r[0]][1] in ("bfloat16", "uint16")
+
+    def copy(o, i, e="v"):
+        dv, da = 0.07 + num(o) * CY * (0.5 if two(o) and two(i) else 1), 0.2 + num(o) * CY
+        return add(e, {"v": dv, "a": da}, [o], [i], lambda e: g.vector.tensor_copy(A(o), A(i)) if e == "v" else
+                   g.scalar.activation(A(o), A(i), AF.Copy))
+
+    def scaled(o, i, k):
+        return add("va", {"v": 0.07 + num(o) * CY, "a": 0.2 + num(o) * CY}, [o], [i],
+                   lambda e: g.vector.tensor_scalar(A(o), A(i), k, None, OP.mult) if e == "v" else
+                   g.scalar.activation(A(o), A(i), AF.Copy, scale=k))
+
+    def ts(o, i, s1, op0, s2=None, op1=None):
+        rd = [i] + [s for s in (s1, s2) if isinstance(s, tuple)]
+        f = lambda s: A(s) if isinstance(s, tuple) else s
+
+        def fn():
+            if op1 is None:
+                return g.vector.tensor_scalar(A(o), A(i), f(s1), None, op0)
+            return g.vector.tensor_scalar(A(o), A(i), f(s1), f(s2), op0, op1)
+        return add("v", 0.07 + num(o) * CY * (0.5 if two(o) and two(i) else 1), [o], rd, fn)
+
+    def tt(o, i, j, op):
+        k = 1 if "ps" in (i[0][:2], j[0][:2]) else 2
+        return add("v", 0.07 + k * num(o) * CY, [o], [i, j], lambda: g.vector.tensor_tensor(A(o), A(i), A(j), op))
+
+    def act(o, i, func, bias=None, scale=1.0):
+        if bias is None:
+            return add("a", 0.2 + num(o) * CY, [o], [i], lambda: g.scalar.activation(A(o), A(i), func, scale=scale))
+        return add("a", 0.2 + num(o) * CY, [o], [i, bias], lambda: g.scalar.activation(A(o), A(i), func, bias=A(bias), scale=scale))
+
+    def mset(o, c):
+        return add("v", 0.07 + num(o) * CY, [o], [], lambda: g.vector.memset(A(o), c))
+
+    def gather(e, o, win, off):
+        f = lambda: A(win).indirect(A(off))
+        d = 0.07 + num(o) * CY * 1.5
+        return add(e, {"v": d, "a": d + 0.1}, [o], [win, off], lambda e: g.vector.tensor_copy(A(o), f()) if e == "v" else
+                   g.scalar.activation(A(o), f(), AF.Copy))
+
+    def mms(lst):
+        w, r, d = [], [], 0.05
+        for o, l, x, s, p in lst:
+            if o not in w:
+                w.append(o)
+            for y in (l, x):
+                if y not in r:
+                    r.append(y)
+            d += max(64, num(x)) * 0.00071 * (4 if not two(x) else 1)
+
+        def fn():
+            z = None
+            for o, l, x, s, p in lst:
+                z = g.tensor.matmul(A(o), A(l), A(x), s, p)
+            return z
+        return add("p", d, w, r, fn)
+
+    def acc(o, pairs):
+        n = len(pairs)
+        return mms([(o, l, x, i == 0, i == n - 1) for i, (l, x) in enumerate(pairs)])
+
+    phys, nbank = {}, [0]
+
+    def bank(kind, n):
+        nbank[0] += 1
+        return ("ps@%d" % nbank[0], 0, n, 1)
+
+    ndma = [0]
+
+    def dma(e, w, r, out, in_, dur=2.0):
+        s = "d%d" % ndma[0]; ndma[0] += 1
+        return add(e, 0.1, w, r, lambda: eng[e].dma_start(out, in_), sem=s, inc=16, lat=dur)
+
+    def iota(o, pattern, base, cm, ints=False):
+        return add("g", 0.15 + num(o) * 2 * CY, [o], [], (lambda: g.iota(A(o), pattern, base, cm)) if ints else
+                   (lambda: g.iota(A(o), pattern, base, cm, allow_small_or_imprecise_dtypes=True)))
+
+    dma("s", [R("XT", 0, W)], [], T.XT[:, 0:W], T.xv[:, :], 6.0)
+    dma("a", [R("wli")], [], T.wli[:, :], T.wl[:, :], 2.5)
+    dma("s", [R("wni")], [], T.wni[0:8, :], T.wn[:, :])
+    dma("a", [R("thi")], [], T.thi[0:8, :], T.th[:, :])
+    dma("s", [R("wti")], [], T.wti[:, :], T.wt[:, :])
+    col = lambda i: R("cols", i, i + 1)
+    PC, LA, GP, G15, K0, L1P, KA, KB, TH, WC, L8, L0, L1, L2, DWC, RC = [col(i) for i in range(16)]
+    iota(R("pint"), [[0, 1]], 0, 1, True); iota(R("XR"), [[1, 144]], 0, 0); iota(R("GR"), [[1, 8], [0, 16]], 0, 0)
+    iota(R("WI"), [[16, 8]], 0, 0); iota(R("YI"), [[1, 52]], -16, 0); iota(R("IO"), [[32, NB]], 0, 0)
+    iota(R("DD"), [[0, 16], [1, 16]], 0, 0); iota(R("DB"), [[1, 16], [0, 16]], 0, 0); iota(R("A16"), [[1, 16]], 0, 0)
+    copy(PC, R("pint")); ts(R("lani"), R("pint"), 15, OP.bitwise_and); ts(R("grpi"), R("pint"), 4, OP.arith_shift_right)
+    copy(LA, R("lani")); copy(GP, R("grpi")); ts(G15, GP, 16.0, OP.mult, 15.0, OP.add)
+    add("v", 0.2, [R("E8")], [R("GR"), PC], lambda: g.vector.tensor_scalar(A(R("E8"), 8), A(R("GR"), 8), A(PC, 8), None, OP.is_equal))
+    add("v", 0.2, [R("wnf", 0, NW)], [R("wni")], lambda: g.vector.tensor_copy(A(R("wnf", 0, NW), 8), A(R("wni"), 8)))
+    add("v", 0.1, [R("wnf", NW, NW + 1)], [R("thi")], lambda: g.vector.tensor_copy(A(R("wnf", NW, NW + 1), 8), A(R("thi"), 8)))
+    bn = bank("n", NW + 1); b0 = bn
+    add("p", 0.4, [b0], [R("E8"), R("wnf")], lambda: g.tensor.matmul(A(bn), A(R("E8"), 8), A(R("wnf"), 8), True, True))
+    copy(R("nr0"), b0)
+    ts(TH, R("nr0", NW, NW + 1), 0.5, OP.add, 200.0, OP.mult)
+    THR = R("nr0", NW, NW + 1)
+    for h in (0, 1):
+        k = col(20 + h)
+        ts(k, LA, float(16 * h), OP.add)
+        ts(R("NLi", h, 2 * NW, 2), R("nr0", 0, NW), k, OP.is_le, float(DEAD), OP.mult)
+    tt(R("NLf"), R("NLi"), R("wli"), OP.max)
+    copy(R("NL"), R("NLf"))
+    mset(R("XT", W, W + 16), 255.0)
+    ts(R("ID"), R("XR", 0, 128), PC, OP.is_equal); ts(R("NEG"), R("XR", 0, 128), PC, OP.is_equal, -1.0, OP.mult)
+    ts(R("BLK"), R("GR"), GP, OP.is_equal); ts(R("BL16"), R("GR"), GP, OP.is_equal, 0.0625, OP.mult)
+    ts(R("BIG"), R("XR", 0, 128), PC, OP.is_equal, 1024.0, OP.mult); mset(R("ONE"), 1.0)
+    for b in range(NBK):
+        mset(R("V%d" % b, 0, 16), 0.0); mset(R("B%d" % b, ROWS, ROWS + 16), 0.0)
+    for x, v in ((L0, 0.0), (L1, 1.0), (L2, 2.0), (L8, 8.0)):
+        ts(x, LA, v, OP.is_equal)
+    ts(R("DD2"), R("DD"), L0, OP.mult); ts(R("DB2"), R("DB"), L1, OP.mult); tt(R("DP"), R("DD2"), R("DB2"), OP.add)
+    ts(R("A16b"), R("A16"), L2, OP.mult)
+    for a in range(16):
+        act(R("DG", 256 * a, 256 * a + 256), R("DP"), AF.Identity, R("A16b", a, a + 1))
+    mset(R("DG", W, W + 16), 0.0)
+    for i in range(4):
+        ts(R("SE%d" % i), R("XR"), G15, OP.is_equal, 3.0 * 2 ** i, OP.mult)
+    for c in range(8):
+        o = R("GT", 128 * c, 128 * c + 128)
+        add("g", 0.4, [o], [R("BL16")], lambda o=o, c=c: g.affine_select(A(o), A(R("BL16")), [[0, 8], [1, 16]], OP.is_gt, 0.0, -c, 0))
+    for c in range(8):
+        b0 = bank("n", 512); l = []
+        for i in range(4):
+            o = R(b0[0], 128 * i, 128 * i + 128)
+            l += [(o, R("ID"), R("GT", 128 * c, 128 * c + 128), True, False), (o, R("ID"), R("SE%d" % i, 15 - c, 143 - c), False, True)]
+        mms(l)
+        copy(R("QW", 512 * c, 512 * c + 512), b0, "a")
+    ts(K0, LA, 8.0, OP.is_lt)
+    ts(col(22), LA, 4.0, OP.mult, 688.0, OP.add); tt(col(23), col(22), K0, OP.mult)
+    ts(KA, col(23), 32.0, OP.add); ts(KB, col(23), 48.0, OP.add)
+    ts(L1P, LA, 1.0, OP.add)
+    ts(R("VY1"), R("YI"), LA, OP.is_le); ts(R("VY2"), R("YI"), L1P, OP.is_equal, 64.0, OP.mult); tt(R("VY"), R("VY1"), R("VY2"), OP.add)
+    for half in (0, 1):
+        b0 = bank("n", 384); l = []
+        for j in range(8):
+            nib = 8 * half + j; c = 0
+            for p in range(4):
+                c += nib >> p & 1
+                l.append((R(b0[0], 48 * j, 48 * j + 48), R("ID"), R("VY", c, c + 48), p == 0, p == 3))
+        mms(l)
+        copy(R("LUT", 384 * half, 384 * half + 384), b0, "a")
+    copy(WC, R("wti")); ts(R("EW"), R("XR"), G15, OP.is_equal); ts(R("WW"), R("XR"), G15, OP.is_equal, WC, OP.mult)
+    ts(col(24), L1, 16.0, OP.mult); ts(col(25), L2, 256.0, OP.mult); tt(col(26), L0, col(24), OP.add); tt(DWC, col(26), col(25), OP.add)
+    ts(R("DW"), R("XR"), G15, OP.is_equal, DWC, OP.mult); ts(R("L0W"), R("XR"), G15, OP.is_equal, L0, OP.mult)
+    ts(R("TBf"), R("GR"), GP, OP.is_equal, L8, OP.mult); ts(R("AS"), R("XR", 0, 128), 0.0, OP.mult, L0, OP.add)
+    ts(R("roti"), R("pint"), 16.0, OP.add); ts(R("rotj"), R("roti"), 127, OP.bitwise_and); copy(RC, R("rotj"))
+    ts(R("ROT"), R("XR", 0, 128), RC, OP.is_equal); ts(R("ROT4"), R("XR", 0, 128), RC, OP.is_equal, float(DEAD), OP.mult)
+    ts(R("IDF"), R("XR", 0, 128), PC, OP.is_equal); ts(R("IDF4"), R("XR", 0, 128), PC, OP.is_equal, float(DEAD), OP.mult); ts(R("BLK2"), R("GR"), GP, OP.is_equal, 2.0, OP.mult)
+    ts(R("WI1"), R("WI"), LA, OP.add, 31.0, OP.mult); ts(R("WI2"), R("WI"), LA, OP.add, float(W + 16), OP.add)
+    ts(R("wf"), R("WI1"), float(-W - 16), OP.add); copy(R("WI1"), R("wf"))
+    mset(R("AC", 0, 1), -0.375)
+    nloc = [0]
+    win = lambda name, r: R(name, 15 - r, 143 - r)
+    chunks = ROWS // CH
+
+    def transmit(kind, t, b):
+        d = [x[3] for x in messages(rank, nr) if x[:3] == (kind, t, b)][0]
+        sb, lb, sem = names_of(kind, t, b)
+        dst = T.cores[d]; via = relay_of(topo, core, dst, kind)
+        to = dst if via is None else via
+        nloc[0] += emask(topo, core, to)[1]
+        s = add("g", 1.0, [], [R(sb)], lambda: send(g, T, topo, core, to, sb, lb, sem), sem="loc", inc=0)
+        n = [x for q in range(nr) for x in messages(q, nr) if x == (kind, t, b, rank)]
+        src = [q for q in range(nr) if (kind, t, b, rank) in messages(q, nr)][0]
+        v2 = relay_of(topo, T.cores[src], T.cores[rank], kind)
+        k = emask(topo, T.cores[src] if v2 is None else v2, core)[1]
+        add(None, 0.0, [R(lb)], [], None, sem=sem, inc=k, after=[s], lat=HOP1 if via is None else HOP2)
+
+    def merge(b, own, over):
+        tt(R("mg%d" % b), own, over, OP.min)
+        ts(R("pv%d" % b), R("mg%d" % b, 0, NB), float(DEAD), OP.is_lt)
+        b0 = bank("n", NB)
+        acc(b0, [(R("BLK2"), R("pv%d" % b))])
+        copy(R("n%d" % b), b0, "va")
+
+    for t in range(RO):
+        for b in range(NBK):
+            s = str(b)
+            V, B, D, C, Z = "V" + s, "B" + s, "D" + s, "C" + s, "Z" + s
+            if t == 0:
+                for q in range(chunks):
+                    n = 2 * NB // chunks
+                    off = R("NL", 2 * NB * b + n * q, 2 * NB * b + n * q + n)
+                    gather("va", R(V, 16 + CH * q, 16 + CH * q + CH), R("XT", 0, W + 16), off)
+                    gather("va", R(B, CH * q, CH * q + CH), R("DG"), off)
+                copy(R("n" + s), R("nr0", NB * b, NB * b + NB))
+            else:
+                merge(b, R("rcv%d%d0" % (t - 1, b)), R("rcv%d%d1" % (t - 1, b)))
+                ts(R("nm" + s), R("mg" + s), float(DEAD), OP.min)
+                n = NB // chunks
+                for q in range(chunks):
+                    for e in (0, 1):
+                        off = R("nm" + s, NB * e + n * q, NB * e + n * q + n)
+                        gather("va", R(V, 16 + CH * q + e, 16 + CH * q + CH, 2), R("XT", 0, W + 16), off)
+                for e in (0, 1):
+                    gather("va", R(B, e, ROWS, 2), R("DG"), R("nm" + s, NB * e, NB * e + NB))
+            ts(R("is" + s), R("n" + s), float(P), OP.is_lt)
+            for q in range(chunks):
+                x = CH * q
+                f = bank("f", CH)
+                mms([(f, R("ID"), R(V, 16 + x, 16 + x + CH), True, False), (R(f[0], 0, CH, P), R("BIG"), R("ONE"), False, False),
+                     (f, R("NEG"), R(V, 15 + x, 15 + x + CH), False, True)])
+                act(R(D, x, x + CH), f, AF.Abs)
+                f = bank("s", CH)
+                acc(f, [(R("BLK"), R(D, x, x + CH))])
+                o = R(C, x, x + CH)
+                add("va", {"v": 0.07 + CH * CY, "a": 0.2 + CH * CY}, [o], [f, TH, THR],
+                    lambda e, o=o, f=f: g.vector.tensor_scalar(A(o), A(f), A(THR), None, OP.is_le) if e == "v" else
+                    g.scalar.activation(A(o), A(f), AF.Sigmoid, bias=A(TH), scale=-200.0))
+                add("v", 0.07 + CH * CY / 2, [R(Z, x, x + CH)], [R(C, x, x + CH), R(V, 16 + x, 16 + x + CH)],
+                    lambda x=x, C=C, V=V, Z=Z: g.vector.tensor_tensor_scan(A(R(Z, x, x + CH)), A(R(C, x, x + CH)), A(R(V, 16 + x, 16 + x + CH)),
+                                                                           0.0, OP.mult, OP.max))
+            f = bank("n", NB)
+            acc(f, [(R("QW", 128 * k, 128 * k + 128), R(C, k, ROWS, P)) for k in range(1, P)])
+            ts(R("IB" + s), f, -1.0, OP.mult, KA, OP.add)
+            ts(R("ix%d0" % b), f, -1.0, OP.mult, KB, OP.add)
+            f = bank("n", NB)
+            acc(f, [(R("TBf"), R("IB" + s))])
+            tt(R("m" + s), f, R("is" + s), OP.subtract)
+            mo = "mos%d%d" % (t, b)
+            ts(R(mo), R("m" + s), 16.0, OP.min)
+            transmit("mo", t, b)
+            if t < RO - 1:
+                add("v", 0.07 + NB * CY, [R("MS", b, b + 1)], [R("m" + s)],
+                    lambda b=b, s=s: g.vector.tensor_reduce(A(R("MS", b, b + 1)), A(R("m" + s)), AxisListType.X, OP.add))
+        if t < RO - 1:
+            f = bank("n", NBK)
+            acc(f, [(R("AS"), R("MS"))])
+            add("v", 0.07, [R("AT")], [f], lambda f=f: g.vector.tensor_reduce(A(R("AT")), A(f), AxisListType.X, OP.add))
+            copy(R("ATi"), R("AT")); ts(R("ATj"), R("ATi"), 255, OP.bitwise_and); ts(R("AC", t + 1, t + 2), R("ATj"), -0.375, OP.add)
+        for h in (0, 1):
+            for b in range(NBK):
+                s = str(b); u = "%d%d" % (b, h)
+                r = lambda n, lo=0, hi=None, step=1: R(n + u, lo, hi, step)
+                if h == 1:
+                    mr = R("mor%d%d" % (t, b))
+                    tt(R("io" + s), R("IB" + s), mr, OP.add)
+                    copy(r("ix"), R("io" + s))
+                gather("va", r("G"), R("LUT"), r("ix"))
+                f = bank("n", NB)
+                acc(f, [(R("ID"), r("G", c, None, 16)) for c in range(8)])
+                copy(r("Pi"), f)
+                ts(r("si"), r("Pi"), 63, OP.bitwise_and); ts(r("ci"), r("Pi"), 6, OP.arith_shift_right)
+                tt(r("af"), r("si"), R("IO"), OP.add)
+                tt(r("zf"), r("af"), r("ci"), OP.add)
+                ts(r("zo"), r("zf"), -1.0, OP.add)
+                gather("va", r("Zc"), R("Z" + s), r("zo"))
+                copy(r("ao"), r("af"))
+                gather("va", r("Ac"), R("B" + s), r("ao"))
+                ts(r("c6"), r("ci"), 611.0, OP.mult); ts(r("c2"), r("ci"), 2.0, OP.mult, 1.0, OP.add)
+                bad = r("iv")
+                tt(bad, r("si"), R("n" + s), OP.is_ge)
+                if h == 1:
+                    ts(r("iw"), mr, LA, OP.is_gt)
+                    bad = r("iy"); tt(bad, r("iv"), r("iw"), OP.max)
+                f = bank("n", NB)
+                acc(f, [(win("WW", x), r("Zc", x, None, 16)) for x in range(16)])
+                copy(r("ui"), f)
+                scaled(r("t1"), f, 37.0)
+                ts(r("um"), r("ui"), W - 1, OP.bitwise_and)
+                tt(r("t2"), r("t1"), r("c6"), OP.add)
+                tt(r("sq"), r("um"), r("um"), OP.mult)
+                ts(r("qq"), r("sq"), 5, OP.arith_shift_right)
+                tt(r("hh"), r("qq"), r("t2"), OP.add)
+                ts(r("hm"), r("hh"), W - 1, OP.bitwise_and)
+                copy(r("hu"), r("hm"))
+                add("v", 0.07 + 16 * NB * CY * 1.5, [r("D2")], [R("XT", 0, W), r("hu"), r("Zc")],
+                    lambda u=u: g.vector.tensor_tensor(A(R("D2" + u)), A(R("XT", 0, W)).indirect(A(R("hu" + u))), A(R("Zc" + u)), OP.subtract))
+                act(r("AD"), r("D2"), AF.Abs)
+                f = bank("n", NB)
+                acc(f, [(win("DW", x), r("Ac", x, None, 16)) for x in range(16)])
+                tt(r("na"), f, r("c2"), OP.mult)
+                ts(r("NN", 0, NB), r("na"), 0.25, OP.mult, R("AC", t, t + 1), OP.add)
+                f = bank("n", NB)
+                acc(f, [(win("EW", x), r("AD", x, None, 16)) for x in range(16)])
+                tt(r("nc"), f, r("c2"), OP.mult)
+                tt(r("NN", NB, 2 * NB), r("nc"), r("hm"), OP.add)
+                ts(r("NM"), r("NN"), W - 1, OP.bitwise_and)
+                sd = R("snd%d%d%d" % (t, b, h))
+                copy(r("NF"), r("NM"))
+                f = bank("n", 2 * NB); l = []
+                x = ("ROT", "ROT4") if t < RO - 1 else ("IDF", "IDF4")
+                for e in (0, 1):
+                    o = R(f[0], NB * e, NB * e + NB)
+                    l += [(o, R(x[0]), r("NF", NB * e, NB * e + NB), True, False), (o, R(x[1]), bad, False, True)]
+                mms(l)
+                copy(sd, f, "va")
+                if t < RO - 1 or h == 1:
+                    transmit("over" if h else "own", t, b)
+                if h == 0:
+                    z0 = R("ZF", NB * b, NB * b + NB)
+                    copy(z0, r("Zc", 0, None, 16))
+                    ts(R("e2" + s), r("D2", 0, None, 16), 0.5, OP.mult, -0.25, OP.add)
+                    tt(R("VAL", NB * b, NB * b + NB), z0, R("e2" + s), OP.add)
+        f = bank("n", 16)
+        fu, fz = R(f[0], 0, 8), R(f[0], 8, 16)
+        mms([(fu, win("WW", x), R("ZF", x, None, 16), x == 0, x == 15) for x in range(16)] +
+            [(fz, win("L0W", x), R("ZF", x, None, 16), x == 0, x == 15) for x in range(16)])
+        copy(R("wa"), fu); ts(R("wc"), fz, 16.0, OP.is_lt)
+        ts(R("wb"), R("wa"), 31, OP.bitwise_and)
+        tt(R("wd"), R("wb"), R("WI1"), OP.add); tt(R("we"), R("wd"), R("wc"), OP.mult); tt(R("wf"), R("we"), R("WI2"), OP.add)
+        copy(R("WL"), R("wf"))
+        add("v", 0.07 + NW * CY * 3, [R("XT")], [R("VAL"), R("WL")],
+            lambda: g.vector.tensor_copy(A(R("XT")).indirect(A(R("WL"))), A(R("VAL"))))
+    for q in range(4):
+        f = bank("f", 512)
+        acc(f, [(R("ID"), R("XT", 1024 * q + e, 1024 * q + 1024, 2)) for e in (0, 1)])
+        copy(R("YX", 512 * q, 512 * q + 512), f, "a")
+    outs = [dma("s", [("yx", 0, 1, 1)], [R("YX")], T.yx[:, :], T.YX[:, :])]
+    for h in (0, 1):
+        for e in (0, 1):
+            v, x, y, z = [col(28 + i) for i in range(4)]
+            ts(v, LA, 2.0, OP.mult, float(e - 16 * h), OP.add)
+            ts(x, v, 0.0, OP.is_ge); ts(y, v, 15.0, OP.is_le); tt(z, x, y, OP.mult)
+            ts(x, v, G15, OP.add, -14.0, OP.add); tt(y, x, z, OP.mult); ts(v, y, -1.0, OP.add)
+            ts(R("PM%d" % (2 * h + e)), R("XR", 0, 128), v, OP.is_equal)
+    ts(R("P8"), R("XR", 0, 8), GP, OP.is_equal, L0, OP.mult)
+    for b in range(NBK):
+        s = str(b)
+        merge(b, R("snd%d%d0" % (RO - 1, b)), R("rcv%d%d1" % (RO - 1, b)))
+        ts(R("yl1" + s), R("mg" + s), float(DEAD), OP.is_lt); tt(R("yl2" + s), R("yl1" + s), R("mg" + s), OP.mult)
+        f = bank("n", 2 * NB)
+        l = []
+        for h in (0, 1):
+            for e in (0, 1):
+                l.append((R(f[0], h, 2 * NB, 2), R("PM%d" % (2 * h + e)), R("yl2" + s, NB * e, NB * e + NB), e == 0, e == 1))
+        mms(l)
+        copy(R("yl3" + s), f)
+        outs.append(dma("s", [("yl", b, b + 1, 1)], [R("yl3" + s)], T.yl[:, 2 * NB * b:2 * NB * b + 2 * NB], T["yl3" + s][:, :]))
+        f = bank("n", NB)
+        add("p", 0.3, [f], [R("P8"), R("n" + s)], lambda f=f, s=s: g.tensor.matmul(A(f, 8), A(R("P8")), A(R("n" + s)), True, True))
+        add("v", 0.1, [R("yno" + s)], [f], lambda f=f, s=s: g.vector.tensor_copy(A(R("yno" + s), 8), A(f, 8)))
+        outs.append(dma("s", [("yn", b, b + 1, 1)], [R("yno" + s)], T.yn[:, NB * b:NB * b + NB], T["yno" + s][0:8, :]))
+
+    n = len(nodes)
+    users = [[] for _ in range(n)]
+    for i, x in enumerate(nodes):
+        for j in x["deps"]:
+            users[j].append(i)
+    prio = [0.0] * n
+    for i in range(n - 1, -1, -1):
+        x = nodes[i]
+        prio[i] = (min(x["d"].values()) if x["e"] == "va" else x["d"][x["e"]] if x["e"] else 0.0) + x["lat"] + LINK + max([prio[k] for k in users[i]] + [0.0])
+    left = [len(x["deps"]) for x in nodes]
+    ready_at = [0.0] * n
+    free = {"v": 0.0, "a": 0.0, "p": 0.0, "g": 0.0, "s": 0.0}
+    ready = {k: [] for k in free}
+    order = []
+    busy = {k: 0.0 for k in free}
+    bfree = [0.0] * 8
+    blast = [[] for _ in range(8)]
+    buse = {}
+    for i, x in enumerate(nodes):
+        for k in x["banks"]:
+            buse.setdefault(k, []).append(i)
+    bleft = {k: len(v) for k, v in buse.items()}
+
+    def done(i, at):
+        for k in users[i]:
+            ready_at[k] = max(ready_at[k], at)
+            left[k] -= 1
+            if left[k] == 0:
+                release(k)
+
+    def release(k):
+        x = nodes[k]
+        if x["e"] is None:
+            x["t"] = ready_at[k]
+            done(k, ready_at[k] + x["lat"])
+        else:
+            for e in x["e"]:
+                ready[e].append(k)
+
+    for i in range(n):
+        if left[i] == 0 and not nodes[i]["deps"]:
+            release(i)
+    while any(ready.values()):
+        best = None
+        for e in free:
+            for k in ready[e]:
+                st = max(free[e], ready_at[k])
+                x = nodes[k]
+                new = [y for y in x["banks"] if y not in phys]
+                if new:
+                    fr = [z for z in bfree if z is not None]
+                    if not fr:
+                        continue
+                    st = max(st, min(fr))
+                key = (st + (VPEN if len(x["e"]) > 1 and e == "v" else 0.0), -prio[k])
+                if best is None or key < best[0]:
+                    best = (key, e, k)
+        (st, _), e, k = best
+        x = nodes[k]
+        for y in x["e"]:
+            ready[y].remove(k)
+        x["e"] = e
+        x["t"] = st
+        fin = st + x["d"][e]
+        for y in x["banks"]:
+            if y not in phys:
+                z = min([z for z in range(8) if bfree[z] is not None], key=lambda z: bfree[z])
+                phys[y] = z
+                bfree[z] = None
+                x["deps"] = sorted(set(x["deps"] + blast[z]))
+                blast[z] = []
+            bleft[y] -= 1
+            blast[phys[y]].append(k)
+            if bleft[y] == 0:
+                bfree[phys[y]] = fin + LINK
+        free[e] = fin
+        busy[e] += x["d"][e]
+        order.append(k)
+        done(k, fin + x["lat"] + LINK)
+    if "want_est" in T.tables:
+        T.tables["want_est"].append((max(free.values()), busy, n, [(x["e"], x.get("t", 0), x["d"].get(x["e"], 0), x) for x in nodes]))
+    cnt = {"v": 0, "a": 0, "p": 0, "g": 0}
+    for k in order:
+        x = nodes[k]
+        if x["sem"] is None:
+            cnt[x["e"]] += 1
+            x["at"] = (esem[x["e"]], cnt[x["e"]])
+        else:
+            x["at"] = (x["sem"], x["inc"])
+    for x in nodes:
+        if x["e"] is None:
+            x["at"] = (x["sem"], x["inc"])
+    known = {k: {} for k in free}
+    for k in order:
+        x = nodes[k]
+        q = eng[x["e"]]
+        need = {}
+        for j in x["deps"]:
+            sm, v = nodes[j]["at"]
+            if sm != "loc":
+                need[sm] = max(need.get(sm, 0), v)
+        for sm in sorted(need):
+            if known[x["e"]].get(sm, 0) < need[sm]:
+                q.wait_ge(T.sem[sm], need[sm])
+                known[x["e"]][sm] = need[sm]
+        z = x["fn"](x["e"])
+        if x["sem"] is None:
+            z.then_inc(T.sem[esem[x["e"]]], 1)
+        elif x["sem"] != "loc":
+            z.then_inc(T.sem[x["sem"]], x["inc"])
+    for e in ("v", "a", "p", "g"):
+        g.wait_ge(T.sem[esem[e]], cnt[e])
+    for i in range(ndma[0]):
+        g.wait_ge(T.sem["d%d" % i], 16)
+    g.wait_ge(T.sem["loc"], nloc[0])

@@ -18,7 +18,7 @@ for _i in range(8):
 
 
 SIZE, PLACE, FILL = {}, {}, {"float32": 0, "int32": 0, "uint16": 0, "bfloat16": 0}
-OWN = ("XT", "wli", "wni", "thi", "wti", "YX", "snd", "rcv", "mos", "mor", "yl3", "yno")
+OWN = ("DG", "HT", "XT0", "XT1", "XT2", "wli", "wni", "thi", "wti", "YX", "snd", "rcv", "mos", "mor", "yl3", "yno")
 
 
 def _sb(name, n, dtype):
@@ -31,22 +31,24 @@ def _sb(name, n, dtype):
         FILL[dtype] += -(-n // 16) * 16
 
 
-_sb("XT", W + 16 + 128, "bfloat16"); _sb("DG", W + 16, "bfloat16"); _sb("LUT", 768, "bfloat16"); _sb("QW", 4096, "bfloat16")
+for _i in range(RO):
+    _sb("XT%d" % _i, W + 16 + 128, "bfloat16")
+_sb("DG", W + 16, "bfloat16"); _sb("LUT", 1552, "bfloat16"); _sb("QW", 4096, "bfloat16")
 _sb("wli", 2 * NW, "int32"); _sb("wni", NW, "int32"); _sb("thi", 1, "int32"); _sb("wti", 1, "int32")
 _sb("wnf", NW + 1, "float32"); _sb("E8", 128, "float32"); _sb("nr0", NW + 1, "float32")
 _sb("pint", 1, "int32"); _sb("lani", 1, "int32"); _sb("grpi", 1, "int32"); _sb("roti", 1, "int32"); _sb("rotj", 1, "int32")
 _sb("cols", 40, "float32")
-_sb("XR", 144, "float32"); _sb("GR", 128, "float32"); _sb("YI", 52, "float32"); _sb("IO", NB, "float32")
+_sb("XR", 144, "float32"); _sb("GR", 128, "float32"); _sb("YI", 52, "float32"); _sb("IO", NB, "bfloat16")
+_sb("E1", 144, "bfloat16"); _sb("E2", 144, "bfloat16"); _sb("E3", 144, "bfloat16"); _sb("OB", 128, "bfloat16"); _sb("OF", 128, "float32"); _sb("L0B", 1, "bfloat16")
+_sb("SC", 1, "float32"); _sb("mA", NW, "float32")
 _sb("WI", 8, "float32"); _sb("WI1", 8, "float32"); _sb("WI2", 8, "float32")
-_sb("DD", 256, "bfloat16"); _sb("DB", 256, "bfloat16"); _sb("DD2", 256, "bfloat16"); _sb("DB2", 256, "bfloat16"); _sb("DP", 256, "bfloat16")
-_sb("A16", 16, "float32"); _sb("A16b", 16, "float32")
-_sb("VY", 52, "bfloat16"); _sb("VY1", 52, "bfloat16"); _sb("VY2", 52, "bfloat16")
+_sb("HT", W, "bfloat16"); _sb("VY", 52, "bfloat16")
 _sb("ID", 128, "bfloat16"); _sb("NEG", 128, "bfloat16"); _sb("BLK", 128, "bfloat16"); _sb("BLK2", 128, "bfloat16"); _sb("BL16", 128, "bfloat16")
 _sb("EW", 144, "bfloat16"); _sb("WW", 144, "bfloat16"); _sb("DW", 144, "bfloat16"); _sb("L0W", 144, "bfloat16")
 for _i in range(4):
     _sb("SE%d" % _i, 144, "bfloat16"); _sb("PM%d" % _i, 128, "float32")
-_sb("GT", 1024, "bfloat16"); _sb("TBf", 128, "float32"); _sb("AS", 128, "float32"); _sb("ROT", 128, "float32"); _sb("ROT4", 128, "float32")
-_sb("IDF", 128, "float32"); _sb("IDF4", 128, "float32"); _sb("BIG", 128, "bfloat16"); _sb("ONE", CH // P, "bfloat16"); _sb("P8", 8, "float32")
+_sb("GT", 1024, "bfloat16"); _sb("TBf", 128, "float32"); _sb("AS", 128, "float32"); _sb("ROT", 128, "float32"); _sb("ROT4", 128, "bfloat16")
+_sb("IDF", 128, "float32"); _sb("IDF4", 128, "bfloat16"); _sb("BIG", 128, "bfloat16"); _sb("ONE", CH // P, "bfloat16"); _sb("P8", 8, "float32")
 _sb("NLi", 2 * NW, "float32"); _sb("NLf", 2 * NW, "float32"); _sb("NL", 2 * NW, "uint16")
 _sb("MS", NBK, "float32"); _sb("AT", 1, "float32"); _sb("ATi", 1, "int32"); _sb("ATj", 1, "int32"); _sb("AC", 4, "float32")
 _sb("ZF", NW, "bfloat16"); _sb("VAL", NW, "bfloat16")
@@ -57,7 +59,7 @@ for _b in range(NBK):
     _s = str(_b)
     _sb("V" + _s, ROWS + 16, "bfloat16"); _sb("B" + _s, ROWS + 16, "bfloat16"); _sb("D" + _s, ROWS, "bfloat16")
     _sb("C" + _s, ROWS, "bfloat16"); _sb("Z" + _s, ROWS, "bfloat16")
-    _sb("n" + _s, NB, "float32"); _sb("is" + _s, NB, "float32"); _sb("m" + _s, NB, "float32"); _sb("IB" + _s, NB, "float32")
+    _sb("n" + _s, NB, "float32"); _sb("nI" + _s, NB, "float32"); _sb("K3" + _s, NB, "float32"); _sb("IB" + _s, NB, "float32")
     _sb("mg" + _s, 2 * NB, "float32"); _sb("nm" + _s, 2 * NB, "uint16"); _sb("pv" + _s, NB, "bfloat16")
     _sb("e2" + _s, NB, "int32"); _sb("io" + _s, NB, "float32")
     _sb("yl1" + _s, 2 * NB, "float32"); _sb("yl2" + _s, 2 * NB, "float32"); _sb("yl3" + _s, 2 * NB, "float32"); _sb("yno" + _s, NB, "float32")
@@ -67,9 +69,8 @@ for _b in range(NBK):
             _sb("snd%d%d%d" % (_t, _b, _h), 2 * NB, "float32"); _sb("rcv%d%d%d" % (_t, _b, _h), 2 * NB, "float32")
     for _h in (0, 1):
         _s = "%d%d" % (_b, _h)
-        for _n, _k, _d in (("ix", NB, "uint16"), ("G", 16 * NB, "bfloat16"), ("Pi", NB, "int32"), ("ci", NB, "int32"), ("si", NB, "int32"),
-                           ("af", NB, "float32"), ("ao", NB, "uint16"), ("zf", NB, "float32"), ("zo", NB, "uint16"), ("iv", NB, "float32"),
-                           ("iw", NB, "float32"), ("iy", NB, "float32"), ("c2", NB, "float32"), ("c6", NB, "float32"), ("Zc", 16 * NB, "bfloat16"),
+        for _n, _k, _d in (("ix", NB, "uint16"), ("G", 16 * NB, "bfloat16"), ("ao", NB, "uint16"), ("zo", NB, "uint16"), ("iv", NB, "bfloat16"),
+                           ("iw", NB, "bfloat16"), ("c2", NB, "float32"), ("c6", NB, "float32"), ("Zc", 16 * NB, "bfloat16"),
                            ("Ac", 16 * NB, "bfloat16"), ("t1", NB, "float32"), ("t2", NB, "float32"), ("ui", NB, "int32"), ("um", NB, "int32"),
                            ("sq", NB, "int32"), ("qq", NB, "int32"), ("hh", NB, "int32"), ("hm", NB, "int32"), ("hu", NB, "uint16"),
                            ("D2", 16 * NB, "bfloat16"), ("AD", 16 * NB, "bfloat16"), ("na", NB, "float32"), ("nc", NB, "float32"),
@@ -81,7 +82,7 @@ for _d in FILL:
     SCRATCH["all_" + _d] = ("sbuf", [128, FILL[_d]], _d)
 
 SEMAPHORES = ["sv", "sa", "st", "sg", "loc"]
-SEMAPHORES += ["d%d" % i for i in range(6 + 2 * NBK)]
+SEMAPHORES += ["d%d" % i for i in range(6 + RO + 2 * NBK)]
 for _t in range(RO):
     for _b in range(NBK):
         SEMAPHORES += ["mo%d%d" % (_t, _b), "nm%d%d0" % (_t, _b), "nm%d%d1" % (_t, _b)]
@@ -89,7 +90,10 @@ for _t in range(RO):
 CY = 0.00083
 HOP1, HOP2 = 3.5, 6.5
 LINK = 0.06
-VPEN = 0.0
+NOISE, SEED = 0.0, 1
+FIRST = 8.0
+GP2 = 2
+VPEN = 0.2
 
 
 def messages(q, n):
@@ -168,6 +172,7 @@ def rank_program(g, core, T, topo):
         return relay_program(g, core, T, topo)
     nr = len(T.cores)
     nodes = []
+    cur = {"plus": 0.0}
     hist = {}
     eng = {"v": g.vector, "a": g.scalar, "p": g.tensor, "g": g, "s": g.sync}
     esem = {"v": "sv", "a": "sa", "p": "st", "g": "sg"}
@@ -199,7 +204,7 @@ def rank_program(g, core, T, topo):
         if not isinstance(dur, dict):
             dur, f1 = {e: dur}, fn
             fn = lambda e: f1()
-        nodes.append({"e": e, "d": dur, "banks": banks, "w": w, "deps": sorted(deps), "fn": fn, "sem": sem, "inc": inc, "lat": lat})
+        nodes.append({"e": e, "d": dur, "plus": cur["plus"], "banks": banks, "w": w, "deps": sorted(deps), "fn": fn, "sem": sem, "inc": inc, "lat": lat})
         return i
 
     def A(r, rows=None):
@@ -291,16 +296,18 @@ def rank_program(g, core, T, topo):
         return add("g", 0.15 + num(o) * 2 * CY, [o], [], (lambda: g.iota(A(o), pattern, base, cm)) if ints else
                    (lambda: g.iota(A(o), pattern, base, cm, allow_small_or_imprecise_dtypes=True)))
 
-    dma("s", [R("XT", 0, W)], [], T.XT[:, 0:W], T.xv[:, :], 6.0)
+    dma("s", [R("XT0", 0, W)], [], T.XT0[:, 0:W], T.xv[:, :], 6.0)
     dma("a", [R("wli")], [], T.wli[:, :], T.wl[:, :], 2.5)
     dma("s", [R("wni")], [], T.wni[0:8, :], T.wn[:, :])
     dma("a", [R("thi")], [], T.thi[0:8, :], T.th[:, :])
     dma("s", [R("wti")], [], T.wti[:, :], T.wt[:, :])
+    for x in range(1, RO):
+        dma("s", [R("XT%d" % x, 0, W)], [R("XT0", 0, W)], T["XT%d" % x][:, 0:W], T.XT0[:, 0:W], 6.0)
     col = lambda i: R("cols", i, i + 1)
-    PC, LA, GP, G15, K0, L1P, KA, KB, TH, WC, L8, L0, L1, L2, DWC, RC = [col(i) for i in range(16)]
+    PC, LA, GP, G15, K0, L1P, KA, KB, TH, WC, NLA, L0, L1, L2, DWC, RC = [col(i) for i in range(16)]
     iota(R("pint"), [[0, 1]], 0, 1, True); iota(R("XR"), [[1, 144]], 0, 0); iota(R("GR"), [[1, 8], [0, 16]], 0, 0)
-    iota(R("WI"), [[16, 8]], 0, 0); iota(R("YI"), [[1, 52]], -16, 0); iota(R("IO"), [[32, NB]], 0, 0)
-    iota(R("DD"), [[0, 16], [1, 16]], 0, 0); iota(R("DB"), [[1, 16], [0, 16]], 0, 0); iota(R("A16"), [[1, 16]], 0, 0)
+    iota(R("WI"), [[16, 8]], 0, 0); iota(R("YI"), [[1, 52]], -17, 0); iota(R("IO"), [[32, NB]], 0, 0)
+    iota(R("DG", 0, W), [[0, 256], [1, 16]], 0, 0); iota(R("HT"), [[1, 256], [0, 16]], 0, 0)
     copy(PC, R("pint")); ts(R("lani"), R("pint"), 15, OP.bitwise_and); ts(R("grpi"), R("pint"), 4, OP.arith_shift_right)
     copy(LA, R("lani")); copy(GP, R("grpi")); ts(G15, GP, 16.0, OP.mult, 15.0, OP.add)
     add("v", 0.2, [R("E8")], [R("GR"), PC], lambda: g.vector.tensor_scalar(A(R("E8"), 8), A(R("GR"), 8), A(PC, 8), None, OP.is_equal))
@@ -317,49 +324,52 @@ def rank_program(g, core, T, topo):
         ts(R("NLi", h, 2 * NW, 2), R("nr0", 0, NW), k, OP.is_le, float(DEAD), OP.mult)
     tt(R("NLf"), R("NLi"), R("wli"), OP.max)
     copy(R("NL"), R("NLf"))
-    mset(R("XT", W, W + 16), 255.0)
+    for x in range(RO):
+        mset(R("XT%d" % x, W, W + 16), 255.0)
     ts(R("ID"), R("XR", 0, 128), PC, OP.is_equal); ts(R("NEG"), R("XR", 0, 128), PC, OP.is_equal, -1.0, OP.mult)
     ts(R("BLK"), R("GR"), GP, OP.is_equal); ts(R("BL16"), R("GR"), GP, OP.is_equal, 0.0625, OP.mult)
     ts(R("BIG"), R("XR", 0, 128), PC, OP.is_equal, 1024.0, OP.mult); mset(R("ONE"), 1.0)
     for b in range(NBK):
         mset(R("V%d" % b, 0, 16), 0.0); mset(R("B%d" % b, ROWS, ROWS + 16), 0.0)
-    for x, v in ((L0, 0.0), (L1, 1.0), (L2, 2.0), (L8, 8.0)):
+    dma("s", [R("DG", 0, W)], [R("HT"), R("DG", 0, W)], T.DG[1::16, 0:W], T.HT[1::16, :], 3.0)
+    for x, v in ((L0, 0.0), (L1, 1.0)):
         ts(x, LA, v, OP.is_equal)
-    ts(R("DD2"), R("DD"), L0, OP.mult); ts(R("DB2"), R("DB"), L1, OP.mult); tt(R("DP"), R("DD2"), R("DB2"), OP.add)
-    ts(R("A16b"), R("A16"), L2, OP.mult)
-    for a in range(16):
-        act(R("DG", 256 * a, 256 * a + 256), R("DP"), AF.Identity, R("A16b", a, a + 1))
     mset(R("DG", W, W + 16), 0.0)
+    ts(R("E1"), R("XR"), G15, OP.is_equal); ts(col(24), G15, 8.0, OP.add); ts(R("E2"), R("XR"), col(24), OP.is_equal)
+    tt(R("E3"), R("E1"), R("E2"), OP.add)
     for i in range(4):
-        ts(R("SE%d" % i), R("XR"), G15, OP.is_equal, 3.0 * 2 ** i, OP.mult)
+        ts(R("SE%d" % i), R("E3"), 3.0 * 2 ** i, OP.mult)
     for c in range(8):
         o = R("GT", 128 * c, 128 * c + 128)
-        add("g", 0.4, [o], [R("BL16")], lambda o=o, c=c: g.affine_select(A(o), A(R("BL16")), [[0, 8], [1, 16]], OP.is_gt, 0.0, -c, 0))
+        add("g", 0.4, [o], [R("BL16")], lambda o=o, c=c: g.affine_select(A(o), A(R("BL16")), [[0, 16], [1, 8]], OP.is_gt, 0.0, -c, 0))
     for c in range(8):
         b0 = bank("n", 512); l = []
         for i in range(4):
             o = R(b0[0], 128 * i, 128 * i + 128)
             l += [(o, R("ID"), R("GT", 128 * c, 128 * c + 128), True, False), (o, R("ID"), R("SE%d" % i, 15 - c, 143 - c), False, True)]
         mms(l)
-        copy(R("QW", 512 * c, 512 * c + 512), b0, "a")
-    ts(K0, LA, 8.0, OP.is_lt)
-    ts(col(22), LA, 4.0, OP.mult, 688.0, OP.add); tt(col(23), col(22), K0, OP.mult)
-    ts(KA, col(23), 32.0, OP.add); ts(KB, col(23), 48.0, OP.add)
-    ts(L1P, LA, 1.0, OP.add)
-    ts(R("VY1"), R("YI"), LA, OP.is_le); ts(R("VY2"), R("YI"), L1P, OP.is_equal, 64.0, OP.mult); tt(R("VY"), R("VY1"), R("VY2"), OP.add)
-    for half in (0, 1):
+        copy(R("QW", 512 * c, 512 * c + 512), b0, "va")
+    ts(K0, LA, 8.0, OP.is_ge, 736.0, OP.mult)
+    ts(col(22), LA, 4.0, OP.mult, 737.0, OP.add); tt(KA, col(22), K0, OP.add); ts(KB, KA, 16.0, OP.add)
+    ts(R("VY"), R("YI"), LA, OP.is_le)
+    for part in range(2):
         b0 = bank("n", 384); l = []
         for j in range(8):
-            nib = 8 * half + j; c = 0
+            nib = 8 * part + j; c = 0
             for p in range(4):
                 c += nib >> p & 1
                 l.append((R(b0[0], 48 * j, 48 * j + 48), R("ID"), R("VY", c, c + 48), p == 0, p == 3))
         mms(l)
-        copy(R("LUT", 384 * half, 384 * half + 384), b0, "a")
+        copy(R("LUT", 16 + 384 * part, 400 + 384 * part), b0, "va")
+    mset(R("LUT", 0, 16), 0.0)
+    for part in range(2):
+        b0 = bank("n", 384); x = 16 + 384 * part
+        acc(b0, [(R("ID"), R("LUT", x - 1, x + 383)), (R("NEG"), R("LUT", x, x + 384))])
+        copy(R("LUT", 768 + x, 1152 + x), b0, "va")
+    mset(R("OB"), 1.0 / 128); mset(R("OF"), 1.0); copy(R("L0B", 0, 1), L0); ts(NLA, LA, -1.0, OP.mult)
     copy(WC, R("wti")); ts(R("EW"), R("XR"), G15, OP.is_equal); ts(R("WW"), R("XR"), G15, OP.is_equal, WC, OP.mult)
-    ts(col(24), L1, 16.0, OP.mult); ts(col(25), L2, 256.0, OP.mult); tt(col(26), L0, col(24), OP.add); tt(DWC, col(26), col(25), OP.add)
+    ts(col(25), L1, 16.0, OP.mult); tt(DWC, L0, col(25), OP.add)
     ts(R("DW"), R("XR"), G15, OP.is_equal, DWC, OP.mult); ts(R("L0W"), R("XR"), G15, OP.is_equal, L0, OP.mult)
-    ts(R("TBf"), R("GR"), GP, OP.is_equal, L8, OP.mult); ts(R("AS"), R("XR", 0, 128), 0.0, OP.mult, L0, OP.add)
     ts(R("roti"), R("pint"), 16.0, OP.add); ts(R("rotj"), R("roti"), 127, OP.bitwise_and); copy(RC, R("rotj"))
     ts(R("ROT"), R("XR", 0, 128), RC, OP.is_equal); ts(R("ROT4"), R("XR", 0, 128), RC, OP.is_equal, float(DEAD), OP.mult)
     ts(R("IDF"), R("XR", 0, 128), PC, OP.is_equal); ts(R("IDF4"), R("XR", 0, 128), PC, OP.is_equal, float(DEAD), OP.mult); ts(R("BLK2"), R("GR"), GP, OP.is_equal, 2.0, OP.mult)
@@ -386,32 +396,37 @@ def rank_program(g, core, T, topo):
     def merge(b, own, over):
         tt(R("mg%d" % b), own, over, OP.min)
         ts(R("pv%d" % b), R("mg%d" % b, 0, NB), float(DEAD), OP.is_lt)
-        b0 = bank("n", NB)
-        acc(b0, [(R("BLK2"), R("pv%d" % b))])
-        copy(R("n%d" % b), b0, "va")
+        b0 = bank("n", 2 * NB)
+        mms([(R(b0[0], 0, NB), R("BLK2"), R("pv%d" % b), True, True), (R(b0[0], NB, 2 * NB), R("BLK2"), R("pv%d" % b), True, False),
+             (R(b0[0], NB, 2 * NB), R("OB"), R("IO"), False, True)])
+        copy(R("n%d" % b), R(b0[0], 0, NB), "va")
+        copy(R("nI%d" % b), R(b0[0], NB, 2 * NB), "va")
 
     for t in range(RO):
+        XT = "XT%d" % t
         for b in range(NBK):
             s = str(b)
+            cur["plus"] = FIRST if b == 0 else 0.0
             V, B, D, C, Z = "V" + s, "B" + s, "D" + s, "C" + s, "Z" + s
             if t == 0:
                 for q in range(chunks):
                     n = 2 * NB // chunks
                     off = R("NL", 2 * NB * b + n * q, 2 * NB * b + n * q + n)
-                    gather("va", R(V, 16 + CH * q, 16 + CH * q + CH), R("XT", 0, W + 16), off)
+                    gather("va", R(V, 16 + CH * q, 16 + CH * q + CH), R(XT, 0, W + 16), off)
                     gather("va", R(B, CH * q, CH * q + CH), R("DG"), off)
-                copy(R("n" + s), R("nr0", NB * b, NB * b + NB))
+                copy(R("n" + s), R("nr0", NB * b, NB * b + NB), "va")
+                tt(R("nI" + s), R("nr0", NB * b, NB * b + NB), R("IO"), OP.add)
             else:
                 merge(b, R("rcv%d%d0" % (t - 1, b)), R("rcv%d%d1" % (t - 1, b)))
                 ts(R("nm" + s), R("mg" + s), float(DEAD), OP.min)
-                n = NB // chunks
-                for q in range(chunks):
+                n = NB // GP2
+                for q in range(GP2):
                     for e in (0, 1):
                         off = R("nm" + s, NB * e + n * q, NB * e + n * q + n)
-                        gather("va", R(V, 16 + CH * q + e, 16 + CH * q + CH, 2), R("XT", 0, W + 16), off)
+                        gather("va", R(V, 16 + P * n * q + e, 16 + P * n * (q + 1), 2), R(XT, 0, W + 16), off)
                 for e in (0, 1):
                     gather("va", R(B, e, ROWS, 2), R("DG"), R("nm" + s, NB * e, NB * e + NB))
-            ts(R("is" + s), R("n" + s), float(P), OP.is_lt)
+            ts(R("K3" + s), R("n" + s), float(P), OP.is_ge, float(P - 1), OP.add)
             for q in range(chunks):
                 x = CH * q
                 f = bank("f", CH)
@@ -428,48 +443,54 @@ def rank_program(g, core, T, topo):
                     lambda x=x, C=C, V=V, Z=Z: g.vector.tensor_tensor_scan(A(R(Z, x, x + CH)), A(R(C, x, x + CH)), A(R(V, 16 + x, 16 + x + CH)),
                                                                            0.0, OP.mult, OP.max))
             f = bank("n", NB)
+            acc(f, [(R("BL16"), R(C, k, ROWS, P)) for k in range(1, P)])
+            mA = R("mA", NB * b, NB * b + NB)
+            tt(mA, R("K3" + s), f, OP.subtract)
+            ts(R("mos%d%d" % (t, b)), mA, 16.0, OP.min)
+            transmit("mo", t, b)
+            f = bank("n", NB)
             acc(f, [(R("QW", 128 * k, 128 * k + 128), R(C, k, ROWS, P)) for k in range(1, P)])
             ts(R("IB" + s), f, -1.0, OP.mult, KA, OP.add)
             ts(R("ix%d0" % b), f, -1.0, OP.mult, KB, OP.add)
-            f = bank("n", NB)
-            acc(f, [(R("TBf"), R("IB" + s))])
-            tt(R("m" + s), f, R("is" + s), OP.subtract)
-            mo = "mos%d%d" % (t, b)
-            ts(R(mo), R("m" + s), 16.0, OP.min)
-            transmit("mo", t, b)
-            if t < RO - 1:
-                add("v", 0.07 + NB * CY, [R("MS", b, b + 1)], [R("m" + s)],
-                    lambda b=b, s=s: g.vector.tensor_reduce(A(R("MS", b, b + 1)), A(R("m" + s)), AxisListType.X, OP.add))
         if t < RO - 1:
-            f = bank("n", NBK)
-            acc(f, [(R("AS"), R("MS"))])
-            add("v", 0.07, [R("AT")], [f], lambda f=f: g.vector.tensor_reduce(A(R("AT")), A(f), AxisListType.X, OP.add))
-            copy(R("ATi"), R("AT")); ts(R("ATj"), R("ATi"), 255, OP.bitwise_and); ts(R("AC", t + 1, t + 2), R("ATj"), -0.375, OP.add)
+            f = bank("n", 1)
+            acc(f, [(R("mA"), L0)])
+            copy(R("SC"), f, "va")
+            f = bank("n", 1)
+            acc(f, [(R("OF"), R("SC"))])
+            copy(R("ATi"), f)
+            ts(R("ATj"), R("ATi"), 255, OP.bitwise_and); ts(R("AC", t + 1, t + 2), R("ATj"), -0.375, OP.add)
         for h in (0, 1):
             for b in range(NBK):
+                cur["plus"] = FIRST if b == 0 else 0.0
                 s = str(b); u = "%d%d" % (b, h)
                 r = lambda n, lo=0, hi=None, step=1: R(n + u, lo, hi, step)
                 if h == 1:
                     mr = R("mor%d%d" % (t, b))
-                    tt(R("io" + s), R("IB" + s), mr, OP.add)
-                    copy(r("ix"), R("io" + s))
+                    f = bank("n", NB)
+                    acc(f, [(R("IDF"), R("IB" + s)), (R("ID"), mr)])
+                    copy(r("ix"), f)
                 gather("va", r("G"), R("LUT"), r("ix"))
-                f = bank("n", NB)
-                acc(f, [(R("ID"), r("G", c, None, 16)) for c in range(8)])
-                copy(r("Pi"), f)
-                ts(r("si"), r("Pi"), 63, OP.bitwise_and); ts(r("ci"), r("Pi"), 6, OP.arith_shift_right)
-                tt(r("af"), r("si"), R("IO"), OP.add)
-                tt(r("zf"), r("af"), r("ci"), OP.add)
-                ts(r("zo"), r("zf"), -1.0, OP.add)
-                gather("va", r("Zc"), R("Z" + s), r("zo"))
-                copy(r("ao"), r("af"))
-                gather("va", r("Ac"), R("B" + s), r("ao"))
-                ts(r("c6"), r("ci"), 611.0, OP.mult); ts(r("c2"), r("ci"), 2.0, OP.mult, 1.0, OP.add)
+                f = bank("n", 3 * NB)
+                fs, fe, fc = R(f[0], 0, NB), R(f[0], NB, 2 * NB), R(f[0], 2 * NB, 3 * NB)
+                bias = [(R("OB"), R("IO"))]
+                ps = [(R("ID"), r("G", c, None, 16)) for c in range(16)]
+                l = []
+                for o, x in ((fe, ps + bias), (fs, ps[:8] + bias), (fc, ps[8:])):
+                    l += [(o, y, z, i == 0, i == len(x) - 1) for i, (y, z) in enumerate(x)]
+                mms(l)
+                ts(r("zo"), fe, -1.0, OP.add)
                 bad = r("iv")
-                tt(bad, r("si"), R("n" + s), OP.is_ge)
+                tt(bad, fs, R("nI" + s), OP.is_ge)
+                copy(r("ao"), fs)
+                scaled(r("c6"), fc, 611.0)
+                add("va", {"v": 0.07 + NB * CY, "a": 0.2 + NB * CY}, [r("c2")], [fc],
+                    lambda e, o=r("c2"), f=fc: g.vector.tensor_scalar(A(o), A(f), 2.0, 1.0, OP.mult, OP.add) if e == "v" else
+                    g.scalar.activation(A(o), A(f), AF.Copy, bias=1.0, scale=2.0))
                 if h == 1:
-                    ts(r("iw"), mr, LA, OP.is_gt)
-                    bad = r("iy"); tt(bad, r("iv"), r("iw"), OP.max)
+                    act(r("iw"), mr, AF.Relu, NLA)
+                gather("va", r("Zc"), R("Z" + s), r("zo"))
+                gather("va", r("Ac"), R("B" + s), r("ao"))
                 f = bank("n", NB)
                 acc(f, [(win("WW", x), r("Zc", x, None, 16)) for x in range(16)])
                 copy(r("ui"), f)
@@ -481,8 +502,8 @@ def rank_program(g, core, T, topo):
                 tt(r("hh"), r("qq"), r("t2"), OP.add)
                 ts(r("hm"), r("hh"), W - 1, OP.bitwise_and)
                 copy(r("hu"), r("hm"))
-                add("v", 0.07 + 16 * NB * CY * 1.5, [r("D2")], [R("XT", 0, W), r("hu"), r("Zc")],
-                    lambda u=u: g.vector.tensor_tensor(A(R("D2" + u)), A(R("XT", 0, W)).indirect(A(R("hu" + u))), A(R("Zc" + u)), OP.subtract))
+                add("v", 0.07 + 16 * NB * CY * 1.5, [r("D2")], [R(XT, 0, W), r("hu"), r("Zc")],
+                    lambda u=u, XT=XT: g.vector.tensor_tensor(A(R("D2" + u)), A(R(XT, 0, W)).indirect(A(R("hu" + u))), A(R("Zc" + u)), OP.subtract))
                 act(r("AD"), r("D2"), AF.Abs)
                 f = bank("n", NB)
                 acc(f, [(win("DW", x), r("Ac", x, None, 16)) for x in range(16)])
@@ -491,7 +512,7 @@ def rank_program(g, core, T, topo):
                 f = bank("n", NB)
                 acc(f, [(win("EW", x), r("AD", x, None, 16)) for x in range(16)])
                 tt(r("nc"), f, r("c2"), OP.mult)
-                tt(r("NN", NB, 2 * NB), r("nc"), r("hm"), OP.add)
+                tt(r("NN", NB, 2 * NB), r("nc"), r("hh"), OP.add)
                 ts(r("NM"), r("NN"), W - 1, OP.bitwise_and)
                 sd = R("snd%d%d%d" % (t, b, h))
                 copy(r("NF"), r("NM"))
@@ -499,16 +520,19 @@ def rank_program(g, core, T, topo):
                 x = ("ROT", "ROT4") if t < RO - 1 else ("IDF", "IDF4")
                 for e in (0, 1):
                     o = R(f[0], NB * e, NB * e + NB)
-                    l += [(o, R(x[0]), r("NF", NB * e, NB * e + NB), True, False), (o, R(x[1]), bad, False, True)]
+                    l += [(o, R(x[0]), r("NF", NB * e, NB * e + NB), True, False), (o, R(x[1]), bad, False, h == 0)]
+                    if h == 1:
+                        l.append((o, R(x[1]), r("iw"), False, True))
                 mms(l)
                 copy(sd, f, "va")
                 if t < RO - 1 or h == 1:
                     transmit("over" if h else "own", t, b)
                 if h == 0:
                     z0 = R("ZF", NB * b, NB * b + NB)
-                    copy(z0, r("Zc", 0, None, 16))
+                    copy(z0, r("Zc", 0, None, 16), "va")
                     ts(R("e2" + s), r("D2", 0, None, 16), 0.5, OP.mult, -0.25, OP.add)
                     tt(R("VAL", NB * b, NB * b + NB), z0, R("e2" + s), OP.add)
+        cur["plus"] = 0.0
         f = bank("n", 16)
         fu, fz = R(f[0], 0, 8), R(f[0], 8, 16)
         mms([(fu, win("WW", x), R("ZF", x, None, 16), x == 0, x == 15) for x in range(16)] +
@@ -517,11 +541,13 @@ def rank_program(g, core, T, topo):
         ts(R("wb"), R("wa"), 31, OP.bitwise_and)
         tt(R("wd"), R("wb"), R("WI1"), OP.add); tt(R("we"), R("wd"), R("wc"), OP.mult); tt(R("wf"), R("we"), R("WI2"), OP.add)
         copy(R("WL"), R("wf"))
-        add("v", 0.07 + NW * CY * 3, [R("XT")], [R("VAL"), R("WL")],
-            lambda: g.vector.tensor_copy(A(R("XT")).indirect(A(R("WL"))), A(R("VAL"))))
+        for x in range(t + 1, RO) if t < RO - 1 else (RO - 1,):
+            o = R("XT%d" % x)
+            add("v", 0.07 + NW * CY * 3, [o], [R("VAL"), R("WL")],
+                lambda o=o: g.vector.tensor_copy(A(o).indirect(A(R("WL"))), A(R("VAL"))))
     for q in range(4):
         f = bank("f", 512)
-        acc(f, [(R("ID"), R("XT", 1024 * q + e, 1024 * q + 1024, 2)) for e in (0, 1)])
+        acc(f, [(R("ID"), R("XT%d" % (RO - 1), 1024 * q + e, 1024 * q + 1024, 2)) for e in (0, 1)])
         copy(R("YX", 512 * q, 512 * q + 512), f, "a")
     outs = [dma("s", [("yx", 0, 1, 1)], [R("YX")], T.yx[:, :], T.YX[:, :])]
     for h in (0, 1):
@@ -558,6 +584,8 @@ def rank_program(g, core, T, topo):
     for i in range(n - 1, -1, -1):
         x = nodes[i]
         prio[i] = (min(x["d"].values()) if x["e"] == "va" else x["d"][x["e"]] if x["e"] else 0.0) + x["lat"] + LINK + max([prio[k] for k in users[i]] + [0.0])
+    for i in range(n):
+        prio[i] += nodes[i]["plus"] + NOISE * ((i * SEED) % 997) / 997.0
     left = [len(x["deps"]) for x in nodes]
     ready_at = [0.0] * n
     free = {"v": 0.0, "a": 0.0, "p": 0.0, "g": 0.0, "s": 0.0}
@@ -605,8 +633,8 @@ def rank_program(g, core, T, topo):
                     st = max(st, min(fr))
                 key = (st + (VPEN if len(x["e"]) > 1 and e == "v" else 0.0), -prio[k])
                 if best is None or key < best[0]:
-                    best = (key, e, k)
-        (st, _), e, k = best
+                    best = (key, e, k, st)
+        _, e, k, st = best
         x = nodes[k]
         for y in x["e"]:
             ready[y].remove(k)

import numpy as np
from concourse.bass import DstId, RemoteDMATransfer
from concourse.mybir import dt, AluOpType, AxisListType, ActivationFunctionType

NW, P, RO = 128, 32, 3
NB = 64
NBK = NW // NB
W = 4096
DEAD = 4096
ROWS = P * NB
CH = 512
AF = ActivationFunctionType
OP = AluOpType

SCRATCH = {}
for _i in range(8):
    SCRATCH["ps%d" % _i] = ("psum", [128, 512], "float32")


SIZE, PLACE, FILL = {}, {}, {"float32": 0, "int32": 0, "uint16": 0, "bfloat16": 0}
OWN = ("DG", "HT", "XT0", "XT1", "XT2", "wli", "wni", "thi", "wti", "YX", "snd", "rcv", "mos", "mor", "yl3", "yno")


def _sb(name, n, dtype):
    SIZE[name] = (n, dtype)
    if name[:3] in OWN or name in OWN:
        SCRATCH[name] = ("sbuf", [128, n], dtype)
        PLACE[name] = (name, 0)
    else:
        PLACE[name] = ("all_" + dtype, FILL[dtype])
        FILL[dtype] += -(-n // 16) * 16


for _i in range(RO):
    _sb("XT%d" % _i, W + 16 + 128, "bfloat16")
_sb("DG", W + 16, "bfloat16"); _sb("LUT", 1552, "bfloat16"); _sb("QW", 4096, "bfloat16")
_sb("wli", 2 * NW, "int32"); _sb("wni", NW, "int32"); _sb("thi", 1, "int32"); _sb("wti", 1, "int32")
_sb("wnf", NW + 1, "float32"); _sb("E8", 128, "float32"); _sb("nr0", NW + 1, "float32")
_sb("pint", 1, "int32"); _sb("lani", 1, "int32"); _sb("grpi", 1, "int32"); _sb("roti", 1, "int32"); _sb("rotj", 1, "int32")
_sb("cols", 40, "float32")
_sb("XR", 144, "float32"); _sb("GR", 128, "float32"); _sb("YI", 52, "float32"); _sb("IO", NB, "bfloat16")
_sb("E1", 144, "bfloat16"); _sb("E2", 144, "bfloat16"); _sb("E3", 144, "bfloat16"); _sb("OB", 128, "bfloat16"); _sb("OF", 128, "float32"); _sb("L0B", 1, "bfloat16")
_sb("SC", 1, "float32"); _sb("mA", NW, "float32")
_sb("WI", 8, "float32"); _sb("WI1", 8, "float32"); _sb("WI2", 8, "float32")
_sb("HT", W, "bfloat16"); _sb("VY", 52, "bfloat16")
_sb("ID", 128, "bfloat16"); _sb("NEG", 128, "bfloat16"); _sb("BLK", 128, "bfloat16"); _sb("BLK2", 128, "bfloat16"); _sb("BL16", 128, "bfloat16")
_sb("EW", 144, "bfloat16"); _sb("WW", 144, "bfloat16"); _sb("DW", 144, "bfloat16"); _sb("L0W", 144, "bfloat16")
for _i in range(4):
    _sb("SE%d" % _i, 144, "bfloat16"); _sb("PM%d" % _i, 128, "float32")
_sb("GT", 1024, "bfloat16"); _sb("TBf", 128, "float32"); _sb("AS", 128, "float32"); _sb("ROT", 128, "float32"); _sb("ROT4", 128, "bfloat16")
_sb("IDF", 128, "float32"); _sb("IDF4", 128, "bfloat16"); _sb("BIG", 128, "bfloat16"); _sb("ONE", CH // P, "bfloat16"); _sb("P8", 8, "float32")
_sb("NLi", 2 * NW, "float32"); _sb("NLf", 2 * NW, "float32"); _sb("NL", 2 * NW, "uint16")
_sb("MS", NBK, "float32"); _sb("AT", 1, "float32"); _sb("ATi", 1, "int32"); _sb("ATj", 1, "int32"); _sb("AC", 4, "float32")
_sb("ZF", NW, "bfloat16"); _sb("VAL", NW, "bfloat16")
for _n, _d in (("wa", "int32"), ("wb", "int32"), ("wc", "float32"), ("wd", "float32"), ("we", "float32"), ("wf", "float32")):
    _sb(_n, 8, _d)
_sb("WL", 8, "uint16"); _sb("YX", 2048, "bfloat16")
for _b in range(NBK):
    _s = str(_b)
    _sb("V" + _s, ROWS + 16, "bfloat16"); _sb("B" + _s, ROWS + 16, "bfloat16"); _sb("D" + _s, ROWS, "bfloat16")
    _sb("C" + _s, ROWS, "bfloat16"); _sb("Z" + _s, ROWS, "bfloat16")
    _sb("n" + _s, NB, "float32"); _sb("nI" + _s, NB, "float32"); _sb("K3" + _s, NB, "float32"); _sb("IB" + _s, NB, "float32")
    _sb("mg" + _s, 2 * NB, "float32"); _sb("nm" + _s, 2 * NB, "uint16"); _sb("pv" + _s, NB, "bfloat16")
    _sb("e2" + _s, NB, "int32"); _sb("io" + _s, NB, "float32")
    _sb("yl1" + _s, 2 * NB, "float32"); _sb("yl2" + _s, 2 * NB, "float32"); _sb("yl3" + _s, 2 * NB, "float32"); _sb("yno" + _s, NB, "float32")
    for _t in range(RO):
        _sb("mos%d%d" % (_t, _b), NB, "bfloat16"); _sb("mor%d%d" % (_t, _b), NB, "bfloat16")
        for _h in (0, 1):
            _sb("snd%d%d%d" % (_t, _b, _h), 2 * NB, "float32"); _sb("rcv%d%d%d" % (_t, _b, _h), 2 * NB, "float32")
    for _h in (0, 1):
        _s = "%d%d" % (_b, _h)
        for _n, _k, _d in (("ix", NB, "uint16"), ("G", 16 * NB, "bfloat16"), ("ao", NB, "uint16"), ("zo", NB, "uint16"), ("iv", NB, "bfloat16"),
                           ("iw", NB, "bfloat16"), ("c2", NB, "float32"), ("c6", NB, "float32"), ("Zc", 16 * NB, "bfloat16"),
                           ("Ac", 16 * NB, "bfloat16"), ("t1", NB, "float32"), ("t2", NB, "float32"), ("ui", NB, "int32"), ("um", NB, "int32"),
                           ("sq", NB, "int32"), ("qq", NB, "int32"), ("hh", NB, "int32"), ("hm", NB, "int32"), ("hu", NB, "uint16"),
                           ("D2", 16 * NB, "bfloat16"), ("AD", 16 * NB, "bfloat16"), ("na", NB, "float32"), ("nc", NB, "float32"),
                           ("NN", 2 * NB, "int32"), ("NM", 2 * NB, "int32"), ("NF", 2 * NB, "float32")):
            _sb(_n + _s, _k, _d)
for _i in range(8):
    SIZE["ps%d" % _i] = (512, "float32"); PLACE["ps%d" % _i] = ("ps%d" % _i, 0)
for _d in FILL:
    SCRATCH["all_" + _d] = ("sbuf", [128, FILL[_d]], _d)

SEMAPHORES = ["sv", "sa", "st", "sg", "loc"]
SEMAPHORES += ["d%d" % i for i in range(6 + RO + 2 * NBK)]
for _t in range(RO):
    for _b in range(NBK):
        SEMAPHORES += ["mo%d%d" % (_t, _b), "nm%d%d0" % (_t, _b), "nm%d%d1" % (_t, _b)]

CY = 0.00083
HOP1, HOP2 = 3.5, 6.5
LINK = 0.06
NOISE, SEED = 0.0, 1
FIRST = 8.0
GP2 = 2
VPEN = 0.2


def messages(q, n):
    out = []
    for t in range(RO):
        for b in range(NBK):
            out.append(("mo", t, b, (q - 1) % n))
            if t < RO - 1:
                out.append(("own", t, b, (q + 1) % n))
                out.append(("over", t, b, (q + 2) % n))
            else:
                out.append(("over", t, b, (q + 1) % n))
    return out


def names_of(kind, t, b):
    if kind == "mo":
        return "mos%d%d" % (t, b), "mor%d%d" % (t, b), "mo%d%d" % (t, b)
    h = 1 if kind == "over" else 0
    return "snd%d%d%d" % (t, b, h), "rcv%d%d%d" % (t, b, h), "nm%d%d%d" % (t, b, h)


def relay_of(topo, src, dst, kind):
    if topo.may_write(src, dst):
        return None
    c = [x for x in topo.cores_of(src) if x != src and topo.die(x) == topo.die(src) and topo.may_write(x, dst)]
    return c[0] if kind != "mo" else c[-1]


def emask(topo, src, dst, n=8):
    m = 0
    for e in topo.engines(src, dst)[:n]:
        m |= 1 << e
    return m, len(topo.engines(src, dst)[:n])


def send(g, T, topo, core, dst, sbuf, dbuf, sem):
    m, k = emask(topo, core, dst)
    rid, pid = topo.addr(dst, core)
    g.remote_dma(T[dbuf][:, :], T[sbuf][:, :], T.sem[sem], T.sem["loc"], pid, rid, m)
    return k


def relay_program(g, core, T, topo):
    todo = []
    n = len(T.cores)
    for q in range(n):
        for kind, t, b, d in messages(q, n):
            dst = T.cores[d]
            if relay_of(topo, T.cores[q], dst, kind) == core:
                todo.append((t, kind == "over", b, kind, T.cores[q], dst))
    tot = 0
    for t, _, b, kind, src, dst in sorted(todo):
        sb, lb, sem = names_of(kind, t, b)
        g.wait_ge(T.sem[sem], emask(topo, src, core)[1])
        tot += send(g, T, topo, core, dst, lb, lb, sem)
    if tot:
        g.wait_ge(T.sem["loc"], tot)


def clash(a, b):
    if a[0] != b[0]:
        return False
    if a[0][:2] == "ps":
        return True
    if a[2] <= b[1] or b[2] <= a[1]:
        return False
    if a[3] == b[3] and a[3] > 1 and (a[1] - b[1]) % a[3]:
        return False
    return True


def rank_program(g, core, T, topo):
    rank = T.rank_of(core)
    if rank is None:
        return relay_program(g, core, T, topo)
    nr = len(T.cores)
    nodes = []
    cur = {"plus": 0.0}
    hist = {}
    eng = {"v": g.vector, "a": g.scalar, "p": g.tensor, "g": g, "s": g.sync}
    esem = {"v": "sv", "a": "sa", "p": "st", "g": "sg"}

    def add(e, dur, w, r, fn, sem=None, inc=1, after=(), lat=0.0):
        i = len(nodes)
        deps = {}
        for x in r:
            ps = x[0][:2] == "ps"
            for (j, y, k) in hist.get(x[0], ()):
                if (k or ps) and clash(x, y):
                    deps[j] = 1
        for x in w:
            for (j, y, k) in hist.get(x[0], ()):
                if clash(x, y):
                    deps[j] = 1
        for j in after:
            deps[j] = 1
        for x in w:
            h = hist.setdefault(x[0], [])
            h[:] = [z for z in h if not (x[3] == 1 and x[1] <= z[1][1] and z[1][2] <= x[2])] if x[0][:2] != "ps" else []
            h.append((i, x, 1))
        for x in r:
            hist.setdefault(x[0], []).append((i, x, 1 if x[0][:2] == "ps" else 0))
        banks = []
        for x in list(w) + list(r):
            if x[0][:2] == "ps" and x[0] not in banks:
                banks.append(x[0])
        if not isinstance(dur, dict):
            dur, f1 = {e: dur}, fn
            fn = lambda e: f1()
        nodes.append({"e": e, "d": dur, "plus": cur["plus"], "banks": banks, "w": w, "deps": sorted(deps), "fn": fn, "sem": sem, "inc": inc, "lat": lat})
        return i

    def A(r, rows=None):
        n, o = ("ps%d" % phys[r[0]], 0) if r[0][:3] == "ps@" else PLACE[r[0]]
        p = slice(None) if rows is None else slice(0, rows)
        return T[n][p, o + r[1]:o + r[2]:r[3]] if r[3] > 1 else T[n][p, o + r[1]:o + r[2]]

    def R(name, lo=0, hi=None, step=1):
        return (name, lo, SIZE[name][0] if hi is None else hi, step)

    def num(r):
        return -(-(r[2] - r[1]) // r[3])

    def two(r):
        return r[0][:2] != "ps" and SIZE[r[0]][1] in ("bfloat16", "uint16")

    def copy(o, i, e="v"):
        dv, da = 0.07 + num(o) * CY * (0.5 if two(o) and two(i) else 1), 0.2 + num(o) * CY
        return add(e, {"v": dv, "a": da}, [o], [i], lambda e: g.vector.tensor_copy(A(o), A(i)) if e == "v" else
                   g.scalar.activation(A(o), A(i), AF.Copy))

    def scaled(o, i, k):
        return add("va", {"v": 0.07 + num(o) * CY, "a": 0.2 + num(o) * CY}, [o], [i],
                   lambda e: g.vector.tensor_scalar(A(o), A(i), k, None, OP.mult) if e == "v" else
                   g.scalar.activation(A(o), A(i), AF.Copy, scale=k))

    def ts(o, i, s1, op0, s2=None, op1=None):
        rd = [i] + [s for s in (s1, s2) if isinstance(s, tuple)]
        f = lambda s: A(s) if isinstance(s, tuple) else s

        def fn():
            if op1 is None:
                return g.vector.tensor_scalar(A(o), A(i), f(s1), None, op0)
            return g.vector.tensor_scalar(A(o), A(i), f(s1), f(s2), op0, op1)
        return add("v", 0.07 + num(o) * CY * (0.5 if two(o) and two(i) else 1), [o], rd, fn)

    def tt(o, i, j, op):
        k = 1 if "ps" in (i[0][:2], j[0][:2]) else 2
        return add("v", 0.07 + k * num(o) * CY, [o], [i, j], lambda: g.vector.tensor_tensor(A(o), A(i), A(j), op))

    def act(o, i, func, bias=None, scale=1.0):
        if bias is None:
            return add("a", 0.2 + num(o) * CY, [o], [i], lambda: g.scalar.activation(A(o), A(i), func, scale=scale))
        return add("a", 0.2 + num(o) * CY, [o], [i, bias], lambda: g.scalar.activation(A(o), A(i), func, bias=A(bias), scale=scale))

    def mset(o, c):
        return add("v", 0.07 + num(o) * CY, [o], [], lambda: g.vector.memset(A(o), c))

    def gather(e, o, win, off):
        f = lambda: A(win).indirect(A(off))
        d = 0.07 + num(o) * CY * 1.5
        return add(e, {"v": d, "a": d + 0.1}, [o], [win, off], lambda e: g.vector.tensor_copy(A(o), f()) if e == "v" else
                   g.scalar.activation(A(o), f(), AF.Copy))

    def mms(lst):
        w, r, d = [], [], 0.05
        for o, l, x, s, p in lst:
            if o not in w:
                w.append(o)
            for y in (l, x):
                if y not in r:
                    r.append(y)
            d += max(64, num(x)) * 0.00071 * (4 if not two(x) else 1)

        def fn():
            z = None
            for o, l, x, s, p in lst:
                z = g.tensor.matmul(A(o), A(l), A(x), s, p)
            return z
        return add("p", d, w, r, fn)

    def acc(o, pairs):
        n = len(pairs)
        return mms([(o, l, x, i == 0, i == n - 1) for i, (l, x) in enumerate(pairs)])

    phys, nbank = {}, [0]

    def bank(kind, n):
        nbank[0] += 1
        return ("ps@%d" % nbank[0], 0, n, 1)

    ndma = [0]

    def dma(e, w, r, out, in_, dur=2.0):
        s = "d%d" % ndma[0]; ndma[0] += 1
        return add(e, 0.1, w, r, lambda: eng[e].dma_start(out, in_), sem=s, inc=16, lat=dur)

    def iota(o, pattern, base, cm, ints=False):
        return add("g", 0.15 + num(o) * 2 * CY, [o], [], (lambda: g.iota(A(o), pattern, base, cm)) if ints else
                   (lambda: g.iota(A(o), pattern, base, cm, allow_small_or_imprecise_dtypes=True)))

    dma("s", [R("XT0", 0, W)], [], T.XT0[:, 0:W], T.xv[:, :], 6.0)
    dma("a", [R("wli")], [], T.wli[:, :], T.wl[:, :], 2.5)
    dma("s", [R("wni")], [], T.wni[0:8, :], T.wn[:, :])
    dma("a", [R("thi")], [], T.thi[0:8, :], T.th[:, :])
    dma("s", [R("wti")], [], T.wti[:, :], T.wt[:, :])
    for x in range(1, RO):
        dma("s", [R("XT%d" % x, 0, W)], [R("XT0", 0, W)], T["XT%d" % x][:, 0:W], T.XT0[:, 0:W], 6.0)
    col = lambda i: R("cols", i, i + 1)
    PC, LA, GP, G15, K0, L1P, KA, KB, TH, WC, NLA, L0, L1, L2, DWC, RC = [col(i) for i in range(16)]
    iota(R("pint"), [[0, 1]], 0, 1, True); iota(R("XR"), [[1, 144]], 0, 0); iota(R("GR"), [[1, 8], [0, 16]], 0, 0)
    iota(R("WI"), [[16, 8]], 0, 0); iota(R("YI"), [[1, 52]], -17, 0); iota(R("IO"), [[32, NB]], 0, 0)
    iota(R("DG", 0, W), [[0, 256], [1, 16]], 0, 0); iota(R("HT"), [[1, 256], [0, 16]], 0, 0)
    copy(PC, R("pint")); ts(R("lani"), R("pint"), 15, OP.bitwise_and); ts(R("grpi"), R("pint"), 4, OP.arith_shift_right)
    copy(LA, R("lani")); copy(GP, R("grpi")); ts(G15, GP, 16.0, OP.mult, 15.0, OP.add)
    add("v", 0.2, [R("E8")], [R("GR"), PC], lambda: g.vector.tensor_scalar(A(R("E8"), 8), A(R("GR"), 8), A(PC, 8), None, OP.is_equal))
    add("v", 0.2, [R("wnf", 0, NW)], [R("wni")], lambda: g.vector.tensor_copy(A(R("wnf", 0, NW), 8), A(R("wni"), 8)))
    add("v", 0.1, [R("wnf", NW, NW + 1)], [R("thi")], lambda: g.vector.tensor_copy(A(R("wnf", NW, NW + 1), 8), A(R("thi"), 8)))
    bn = bank("n", NW + 1); b0 = bn
    add("p", 0.4, [b0], [R("E8"), R("wnf")], lambda: g.tensor.matmul(A(bn), A(R("E8"), 8), A(R("wnf"), 8), True, True))
    copy(R("nr0"), b0)
    ts(TH, R("nr0", NW, NW + 1), 0.5, OP.add, 200.0, OP.mult)
    THR = R("nr0", NW, NW + 1)
    for h in (0, 1):
        k = col(20 + h)
        ts(k, LA, float(16 * h), OP.add)
        ts(R("NLi", h, 2 * NW, 2), R("nr0", 0, NW), k, OP.is_le, float(DEAD), OP.mult)
    tt(R("NLf"), R("NLi"), R("wli"), OP.max)
    copy(R("NL"), R("NLf"))
    for x in range(RO):
        mset(R("XT%d" % x, W, W + 16), 255.0)
    ts(R("ID"), R("XR", 0, 128), PC, OP.is_equal); ts(R("NEG"), R("XR", 0, 128), PC, OP.is_equal, -1.0, OP.mult)
    ts(R("BLK"), R("GR"), GP, OP.is_equal); ts(R("BL16"), R("GR"), GP, OP.is_equal, 0.0625, OP.mult)
    ts(R("BIG"), R("XR", 0, 128), PC, OP.is_equal, 1024.0, OP.mult); mset(R("ONE"), 1.0)
    for b in range(NBK):
        mset(R("V%d" % b, 0, 16), 0.0); mset(R("B%d" % b, ROWS, ROWS + 16), 0.0)
    dma("s", [R("DG", 0, W)], [R("HT"), R("DG", 0, W)], T.DG[1::16, 0:W], T.HT[1::16, :], 3.0)
    for x, v in ((L0, 0.0), (L1, 1.0)):
        ts(x, LA, v, OP.is_equal)
    mset(R("DG", W, W + 16), 0.0)
    ts(R("E1"), R("XR"), G15, OP.is_equal); ts(col(24), G15, 8.0, OP.add); ts(R("E2"), R("XR"), col(24), OP.is_equal)
    tt(R("E3"), R("E1"), R("E2"), OP.add)
    for i in range(4):
        ts(R("SE%d" % i), R("E3"), 3.0 * 2 ** i, OP.mult)
    for c in range(8):
        o = R("GT", 128 * c, 128 * c + 128)
        add("g", 0.4, [o], [R("BL16")], lambda o=o, c=c: g.affine_select(A(o), A(R("BL16")), [[0, 16], [1, 8]], OP.is_gt, 0.0, -c, 0))
    for c in range(8):
        b0 = bank("n", 512); l = []
        for i in range(4):
            o = R(b0[0], 128 * i, 128 * i + 128)
            l += [(o, R("ID"), R("GT", 128 * c, 128 * c + 128), True, False), (o, R("ID"), R("SE%d" % i, 15 - c, 143 - c), False, True)]
        mms(l)
        copy(R("QW", 512 * c, 512 * c + 512), b0, "va")
    ts(K0, LA, 8.0, OP.is_ge, 736.0, OP.mult)
    ts(col(22), LA, 4.0, OP.mult, 737.0, OP.add); tt(KA, col(22), K0, OP.add); ts(KB, KA, 16.0, OP.add)
    ts(R("VY"), R("YI"), LA, OP.is_le)
    for part in range(2):
        b0 = bank("n", 384); l = []
        for j in range(8):
            nib = 8 * part + j; c = 0
            for p in range(4):
                c += nib >> p & 1
                l.append((R(b0[0], 48 * j, 48 * j + 48), R("ID"), R("VY", c, c + 48), p == 0, p == 3))
        mms(l)
        copy(R("LUT", 16 + 384 * part, 400 + 384 * part), b0, "va")
    mset(R("LUT", 0, 16), 0.0)
    for part in range(2):
        b0 = bank("n", 384); x = 16 + 384 * part
        acc(b0, [(R("ID"), R("LUT", x - 1, x + 383)), (R("NEG"), R("LUT", x, x + 384))])
        copy(R("LUT", 768 + x, 1152 + x), b0, "va")
    mset(R("OB"), 1.0 / 128); mset(R("OF"), 1.0); copy(R("L0B", 0, 1), L0); ts(NLA, LA, -1.0, OP.mult)
    copy(WC, R("wti")); ts(R("EW"), R("XR"), G15, OP.is_equal); ts(R("WW"), R("XR"), G15, OP.is_equal, WC, OP.mult)
    ts(col(25), L1, 16.0, OP.mult); tt(DWC, L0, col(25), OP.add)
    ts(R("DW"), R("XR"), G15, OP.is_equal, DWC, OP.mult); ts(R("L0W"), R("XR"), G15, OP.is_equal, L0, OP.mult)
    ts(R("roti"), R("pint"), 16.0, OP.add); ts(R("rotj"), R("roti"), 127, OP.bitwise_and); copy(RC, R("rotj"))
    ts(R("ROT"), R("XR", 0, 128), RC, OP.is_equal); ts(R("ROT4"), R("XR", 0, 128), RC, OP.is_equal, float(DEAD), OP.mult)
    ts(R("IDF"), R("XR", 0, 128), PC, OP.is_equal); ts(R("IDF4"), R("XR", 0, 128), PC, OP.is_equal, float(DEAD), OP.mult); ts(R("BLK2"), R("GR"), GP, OP.is_equal, 2.0, OP.mult)
    ts(R("WI1"), R("WI"), LA, OP.add, 31.0, OP.mult); ts(R("WI2"), R("WI"), LA, OP.add, float(W + 16), OP.add)
    ts(R("wf"), R("WI1"), float(-W - 16), OP.add); copy(R("WI1"), R("wf"))
    mset(R("AC", 0, 1), -0.375)
    nloc = [0]
    win = lambda name, r: R(name, 15 - r, 143 - r)
    chunks = ROWS // CH

    def transmit(kind, t, b):
        d = [x[3] for x in messages(rank, nr) if x[:3] == (kind, t, b)][0]
        sb, lb, sem = names_of(kind, t, b)
        dst = T.cores[d]; via = relay_of(topo, core, dst, kind)
        to = dst if via is None else via
        nloc[0] += emask(topo, core, to)[1]
        s = add("g", 1.0, [], [R(sb)], lambda: send(g, T, topo, core, to, sb, lb, sem), sem="loc", inc=0)
        n = [x for q in range(nr) for x in messages(q, nr) if x == (kind, t, b, rank)]
        src = [q for q in range(nr) if (kind, t, b, rank) in messages(q, nr)][0]
        v2 = relay_of(topo, T.cores[src], T.cores[rank], kind)
        k = emask(topo, T.cores[src] if v2 is None else v2, core)[1]
        add(None, 0.0, [R(lb)], [], None, sem=sem, inc=k, after=[s], lat=HOP1 if via is None else HOP2)

    def merge(b, own, over):
        tt(R("mg%d" % b), own, over, OP.min)
        ts(R("pv%d" % b), R("mg%d" % b, 0, NB), float(DEAD), OP.is_lt)
        b0 = bank("n", 2 * NB)
        mms([(R(b0[0], 0, NB), R("BLK2"), R("pv%d" % b), True, True), (R(b0[0], NB, 2 * NB), R("BLK2"), R("pv%d" % b), True, False),
             (R(b0[0], NB, 2 * NB), R("OB"), R("IO"), False, True)])
        copy(R("n%d" % b), R(b0[0], 0, NB), "va")
        copy(R("nI%d" % b), R(b0[0], NB, 2 * NB), "va")

    for t in range(RO):
        XT = "XT%d" % t
        for b in range(NBK):
            s = str(b)
            cur["plus"] = FIRST if b == 0 else 0.0
            V, B, D, C, Z = "V" + s, "B" + s, "D" + s, "C" + s, "Z" + s
            if t == 0:
                for q in range(chunks):
                    n = 2 * NB // chunks
                    off = R("NL", 2 * NB * b + n * q, 2 * NB * b + n * q + n)
                    gather("va", R(V, 16 + CH * q, 16 + CH * q + CH), R(XT, 0, W + 16), off)
                    gather("va", R(B, CH * q, CH * q + CH), R("DG"), off)
                copy(R("n" + s), R("nr0", NB * b, NB * b + NB), "va")
                tt(R("nI" + s), R("nr0", NB * b, NB * b + NB), R("IO"), OP.add)
            else:
                merge(b, R("rcv%d%d0" % (t - 1, b)), R("rcv%d%d1" % (t - 1, b)))
                ts(R("nm" + s), R("mg" + s), float(DEAD), OP.min)
                n = NB // GP2
                for q in range(GP2):
                    for e in (0, 1):
                        off = R("nm" + s, NB * e + n * q, NB * e + n * q + n)
                        gather("va", R(V, 16 + P * n * q + e, 16 + P * n * (q + 1), 2), R(XT, 0, W + 16), off)
                for e in (0, 1):
                    gather("va", R(B, e, ROWS, 2), R("DG"), R("nm" + s, NB * e, NB * e + NB))
            ts(R("K3" + s), R("n" + s), float(P), OP.is_ge, float(P - 1), OP.add)
            for q in range(chunks):
                x = CH * q
                f = bank("f", CH)
                mms([(f, R("ID"), R(V, 16 + x, 16 + x + CH), True, False), (R(f[0], 0, CH, P), R("BIG"), R("ONE"), False, False),
                     (f, R("NEG"), R(V, 15 + x, 15 + x + CH), False, True)])
                act(R(D, x, x + CH), f, AF.Abs)
                f = bank("s", CH)
                acc(f, [(R("BLK"), R(D, x, x + CH))])
                o = R(C, x, x + CH)
                add("va", {"v": 0.07 + CH * CY, "a": 0.2 + CH * CY}, [o], [f, TH, THR],
                    lambda e, o=o, f=f: g.vector.tensor_scalar(A(o), A(f), A(THR), None, OP.is_le) if e == "v" else
                    g.scalar.activation(A(o), A(f), AF.Sigmoid, bias=A(TH), scale=-200.0))
                add("v", 0.07 + CH * CY / 2, [R(Z, x, x + CH)], [R(C, x, x + CH), R(V, 16 + x, 16 + x + CH)],
                    lambda x=x, C=C, V=V, Z=Z: g.vector.tensor_tensor_scan(A(R(Z, x, x + CH)), A(R(C, x, x + CH)), A(R(V, 16 + x, 16 + x + CH)),
                                                                           0.0, OP.mult, OP.max))
            f = bank("n", NB)
            acc(f, [(R("BL16"), R(C, k, ROWS, P)) for k in range(1, P)])
            mA = R("mA", NB * b, NB * b + NB)
            tt(mA, R("K3" + s), f, OP.subtract)
            ts(R("mos%d%d" % (t, b)), mA, 16.0, OP.min)
            transmit("mo", t, b)
            f = bank("n", NB)
            acc(f, [(R("QW", 128 * k, 128 * k + 128), R(C, k, ROWS, P)) for k in range(1, P)])
            ts(R("IB" + s), f, -1.0, OP.mult, KA, OP.add)
            ts(R("ix%d0" % b), f, -1.0, OP.mult, KB, OP.add)
        if t < RO - 1:
            f = bank("n", 1)
            acc(f, [(R("mA"), L0)])
            copy(R("SC"), f, "va")
            f = bank("n", 1)
            acc(f, [(R("OF"), R("SC"))])
            copy(R("ATi"), f)
            ts(R("ATj"), R("ATi"), 255, OP.bitwise_and); ts(R("AC", t + 1, t + 2), R("ATj"), -0.375, OP.add)
        for h in (0, 1):
            for b in range(NBK):
                cur["plus"] = FIRST if b == 0 else 0.0
                s = str(b); u = "%d%d" % (b, h)
                r = lambda n, lo=0, hi=None, step=1: R(n + u, lo, hi, step)
                if h == 1:
                    mr = R("mor%d%d" % (t, b))
                    f = bank("n", NB)
                    acc(f, [(R("IDF"), R("IB" + s)), (R("ID"), mr)])
                    copy(r("ix"), f)
                gather("va", r("G"), R("LUT"), r("ix"))
                f = bank("n", 3 * NB)
                fs, fe, fc = R(f[0], 0, NB), R(f[0], NB, 2 * NB), R(f[0], 2 * NB, 3 * NB)
                bias = [(R("OB"), R("IO"))]
                ps = [(R("ID"), r("G", c, None, 16)) for c in range(16)]
                l = []
                for o, x in ((fe, ps + bias), (fs, ps[:8] + bias), (fc, ps[8:])):
                    l += [(o, y, z, i == 0, i == len(x) - 1) for i, (y, z) in enumerate(x)]
                mms(l)
                ts(r("zo"), fe, -1.0, OP.add)
                bad = r("iv")
                tt(bad, fs, R("nI" + s), OP.is_ge)
                copy(r("ao"), fs)
                scaled(r("c6"), fc, 611.0)
                add("va", {"v": 0.07 + NB * CY, "a": 0.2 + NB * CY}, [r("c2")], [fc],
                    lambda e, o=r("c2"), f=fc: g.vector.tensor_scalar(A(o), A(f), 2.0, 1.0, OP.mult, OP.add) if e == "v" else
                    g.scalar.activation(A(o), A(f), AF.Copy, bias=1.0, scale=2.0))
                if h == 1:
                    act(r("iw"), mr, AF.Relu, NLA)
                gather("va", r("Zc"), R("Z" + s), r("zo"))
                gather("va", r("Ac"), R("B" + s), r("ao"))
                f = bank("n", NB)
                acc(f, [(win("WW", x), r("Zc", x, None, 16)) for x in range(16)])
                copy(r("ui"), f)
                scaled(r("t1"), f, 37.0)
                ts(r("um"), r("ui"), W - 1, OP.bitwise_and)
                tt(r("t2"), r("t1"), r("c6"), OP.add)
                tt(r("sq"), r("um"), r("um"), OP.mult)
                ts(r("qq"), r("sq"), 5, OP.arith_shift_right)
                tt(r("hh"), r("qq"), r("t2"), OP.add)
                ts(r("hm"), r("hh"), W - 1, OP.bitwise_and)
                copy(r("hu"), r("hm"))
                add("v", 0.07 + 16 * NB * CY * 1.5, [r("D2")], [R(XT, 0, W), r("hu"), r("Zc")],
                    lambda u=u, XT=XT: g.vector.tensor_tensor(A(R("D2" + u)), A(R(XT, 0, W)).indirect(A(R("hu" + u))), A(R("Zc" + u)), OP.subtract))
                act(r("AD"), r("D2"), AF.Abs)
                f = bank("n", NB)
                acc(f, [(win("DW", x), r("Ac", x, None, 16)) for x in range(16)])
                tt(r("na"), f, r("c2"), OP.mult)
                ts(r("NN", 0, NB), r("na"), 0.25, OP.mult, R("AC", t, t + 1), OP.add)
                f = bank("n", NB)
                acc(f, [(win("EW", x), r("AD", x, None, 16)) for x in range(16)])
                tt(r("nc"), f, r("c2"), OP.mult)
                tt(r("NN", NB, 2 * NB), r("nc"), r("hh"), OP.add)
                ts(r("NM"), r("NN"), W - 1, OP.bitwise_and)
                sd = R("snd%d%d%d" % (t, b, h))
                copy(r("NF"), r("NM"))
                f = bank("n", 2 * NB); l = []
                x = ("ROT", "ROT4") if t < RO - 1 else ("IDF", "IDF4")
                for e in (0, 1):
                    o = R(f[0], NB * e, NB * e + NB)
                    l += [(o, R(x[0]), r("NF", NB * e, NB * e + NB), True, False), (o, R(x[1]), bad, False, h == 0)]
                    if h == 1:
                        l.append((o, R(x[1]), r("iw"), False, True))
                mms(l)
                copy(sd, f, "va")
                if t < RO - 1 or h == 1:
                    transmit("over" if h else "own", t, b)
                if h == 0:
                    z0 = R("ZF", NB * b, NB * b + NB)
                    copy(z0, r("Zc", 0, None, 16), "va")
                    ts(R("e2" + s), r("D2", 0, None, 16), 0.5, OP.mult, -0.25, OP.add)
                    tt(R("VAL", NB * b, NB * b + NB), z0, R("e2" + s), OP.add)
        cur["plus"] = 0.0
        f = bank("n", 16)
        fu, fz = R(f[0], 0, 8), R(f[0], 8, 16)
        mms([(fu, win("WW", x), R("ZF", x, None, 16), x == 0, x == 15) for x in range(16)] +
            [(fz, win("L0W", x), R("ZF", x, None, 16), x == 0, x == 15) for x in range(16)])
        copy(R("wa"), fu); ts(R("wc"), fz, 16.0, OP.is_lt)
        ts(R("wb"), R("wa"), 31, OP.bitwise_and)
        tt(R("wd"), R("wb"), R("WI1"), OP.add); tt(R("we"), R("wd"), R("wc"), OP.mult); tt(R("wf"), R("we"), R("WI2"), OP.add)
        copy(R("WL"), R("wf"))
        for x in range(t + 1, RO) if t < RO - 1 else (RO - 1,):
            o = R("XT%d" % x)
            add("v", 0.07 + NW * CY * 3, [o], [R("VAL"), R("WL")],
                lambda o=o: g.vector.tensor_copy(A(o).indirect(A(R("WL"))), A(R("VAL"))))
    for q in range(4):
        f = bank("f", 512)
        acc(f, [(R("ID"), R("XT%d" % (RO - 1), 1024 * q + e, 1024 * q + 1024, 2)) for e in (0, 1)])
        copy(R("YX", 512 * q, 512 * q + 512), f, "a")
    outs = [dma("s", [("yx", 0, 1, 1)], [R("YX")], T.yx[:, :], T.YX[:, :])]
    for h in (0, 1):
        for e in (0, 1):
            v, x, y, z = [col(28 + i) for i in range(4)]
            ts(v, LA, 2.0, OP.mult, float(e - 16 * h), OP.add)
            ts(x, v, 0.0, OP.is_ge); ts(y, v, 15.0, OP.is_le); tt(z, x, y, OP.mult)
            ts(x, v, G15, OP.add, -14.0, OP.add); tt(y, x, z, OP.mult); ts(v, y, -1.0, OP.add)
            ts(R("PM%d" % (2 * h + e)), R("XR", 0, 128), v, OP.is_equal)
    ts(R("P8"), R("XR", 0, 8), GP, OP.is_equal, L0, OP.mult)
    for b in range(NBK):
        s = str(b)
        merge(b, R("snd%d%d0" % (RO - 1, b)), R("rcv%d%d1" % (RO - 1, b)))
        ts(R("yl1" + s), R("mg" + s), float(DEAD), OP.is_lt); tt(R("yl2" + s), R("yl1" + s), R("mg" + s), OP.mult)
        f = bank("n", 2 * NB)
        l = []
        for h in (0, 1):
            for e in (0, 1):
                l.append((R(f[0], h, 2 * NB, 2), R("PM%d" % (2 * h + e)), R("yl2" + s, NB * e, NB * e + NB), e == 0, e == 1))
        mms(l)
        copy(R("yl3" + s), f)
        outs.append(dma("s", [("yl", b, b + 1, 1)], [R("yl3" + s)], T.yl[:, 2 * NB * b:2 * NB * b + 2 * NB], T["yl3" + s][:, :]))
        f = bank("n", NB)
        add("p", 0.3, [f], [R("P8"), R("n" + s)], lambda f=f, s=s: g.tensor.matmul(A(f, 8), A(R("P8")), A(R("n" + s)), True, True))
        add("v", 0.1, [R("yno" + s)], [f], lambda f=f, s=s: g.vector.tensor_copy(A(R("yno" + s), 8), A(f, 8)))
        outs.append(dma("s", [("yn", b, b + 1, 1)], [R("yno" + s)], T.yn[:, NB * b:NB * b + NB], T["yno" + s][0:8, :]))

    n = len(nodes)
    users = [[] for _ in range(n)]
    for i, x in enumerate(nodes):
        for j in x["deps"]:
            users[j].append(i)
    prio = [0.0] * n
    for i in range(n - 1, -1, -1):
        x = nodes[i]
        prio[i] = (min(x["d"].values()) if x["e"] == "va" else x["d"][x["e"]] if x["e"] else 0.0) + x["lat"] + LINK + max([prio[k] for k in users[i]] + [0.0])
    for i in range(n):
        prio[i] += nodes[i]["plus"] + NOISE * ((i * SEED) % 997) / 997.0
    left = [len(x["deps"]) for x in nodes]
    ready_at = [0.0] * n
    free = {"v": 0.0, "a": 0.0, "p": 0.0, "g": 0.0, "s": 0.0}
    ready = {k: [] for k in free}
    order = []
    busy = {k: 0.0 for k in free}
    bfree = [0.0] * 8
    blast = [[] for _ in range(8)]
    buse = {}
    for i, x in enumerate(nodes):
        for k in x["banks"]:
            buse.setdefault(k, []).append(i)
    bleft = {k: len(v) for k, v in buse.items()}

    def done(i, at):
        for k in users[i]:
            ready_at[k] = max(ready_at[k], at)
            left[k] -= 1
            if left[k] == 0:
                release(k)

    def release(k):
        x = nodes[k]
        if x["e"] is None:
            x["t"] = ready_at[k]
            done(k, ready_at[k] + x["lat"])
        else:
            for e in x["e"]:
                ready[e].append(k)

    for i in range(n):
        if left[i] == 0 and not nodes[i]["deps"]:
            release(i)
    while any(ready.values()):
        best = None
        for e in free:
            for k in ready[e]:
                st = max(free[e], ready_at[k])
                x = nodes[k]
                new = [y for y in x["banks"] if y not in phys]
                if new:
                    fr = [z for z in bfree if z is not None]
                    if not fr:
                        continue
                    st = max(st, min(fr))
                key = (st + (VPEN if len(x["e"]) > 1 and e == "v" else 0.0), -prio[k])
                if best is None or key < best[0]:
                    best = (key, e, k, st)
        _, e, k, st = best
        x = nodes[k]
        for y in x["e"]:
            ready[y].remove(k)
        x["e"] = e
        x["t"] = st
        fin = st + x["d"][e]
        for y in x["banks"]:
            if y not in phys:
                z = min([z for z in range(8) if bfree[z] is not None], key=lambda z: bfree[z])
                phys[y] = z
                bfree[z] = None
                x["deps"] = sorted(set(x["deps"] + blast[z]))
                blast[z] = []
            bleft[y] -= 1
            blast[phys[y]].append(k)
            if bleft[y] == 0:
                bfree[phys[y]] = fin + LINK
        free[e] = fin
        busy[e] += x["d"][e]
        order.append(k)
        done(k, fin + x["lat"] + LINK)
    if "want_est" in T.tables:
        T.tables["want_est"].append((max(free.values()), busy, n, [(x["e"], x.get("t", 0), x["d"].get(x["e"], 0), x) for x in nodes]))
    cnt = {"v": 0, "a": 0, "p": 0, "g": 0}
    for k in order:
        x = nodes[k]
        if x["sem"] is None:
            cnt[x["e"]] += 1
            x["at"] = (esem[x["e"]], cnt[x["e"]])
        else:
            x["at"] = (x["sem"], x["inc"])
    for x in nodes:
        if x["e"] is None:
            x["at"] = (x["sem"], x["inc"])
    known = {k: {} for k in free}
    for k in order:
        x = nodes[k]
        q = eng[x["e"]]
        need = {}
        for j in x["deps"]:
            sm, v = nodes[j]["at"]
            if sm != "loc":
                need[sm] = max(need.get(sm, 0), v)
        for sm in sorted(need):
            if known[x["e"]].get(sm, 0) < need[sm]:
                q.wait_ge(T.sem[sm], need[sm])
                known[x["e"]][sm] = need[sm]
        z = x["fn"](x["e"])
        if x["sem"] is None:
            z.then_inc(T.sem[esem[x["e"]]], 1)
        elif x["sem"] != "loc":
            z.then_inc(T.sem[x["sem"]], x["inc"])
    for e in ("v", "a", "p", "g"):
        g.wait_ge(T.sem[esem[e]], cnt[e])
    for i in range(ndma[0]):
        g.wait_ge(T.sem["d%d" % i], 16)
    g.wait_ge(T.sem["loc"], nloc[0])
